import numpy as np
import ml_dtypes


def mxq(x, axis, fmt="e4m3"):
    dtype, down = {"e4m3": (ml_dtypes.float8_e4m3fn, 7), "e5m2": (ml_dtypes.float8_e5m2, 14)}[fmt]
    v = np.moveaxis(np.asarray(x, np.float32).astype(ml_dtypes.bfloat16).astype(np.float64), axis, -1)
    blocks = v.reshape(v.shape[:-1] + (-1, 32))
    amax = np.abs(blocks).max(-1, keepdims=True)
    byte = np.maximum(np.where(amax > 0, np.frexp(amax)[1] - 1 + 127, 0) - down, 1)
    scale = np.exp2(byte - 127.0)
    codes = (blocks / scale).astype(np.float32).astype(dtype).astype(np.float64)
    return np.moveaxis((codes * scale).reshape(v.shape), -1, axis)


WIDE = False


def mx_kscale(k):
    if not WIDE:
        return np.ones(k)
    levels = np.array([10, -10, 5, -5, 0])
    if k % 512:
        return np.exp2(np.random.permutation(np.resize(levels, k // 32))).repeat(32)
    a = np.empty((k // 512, 16))
    for p in range(k // 512):
        a[p, :8] = np.random.permutation(np.resize(levels, 8))
        for g in range(8):
            far = levels[np.abs(levels - a[p, g]) >= 10]
            a[p, g + 8] = far[np.random.randint(len(far))]
    return np.exp2(a.ravel()).repeat(32)


def f64(x):
    return np.asarray(x).astype(np.float64)


def striped(idx):
    return np.tile(idx.reshape(-1, 16).T, (8, 1)).astype(np.uint16)


def unstriped(offs):
    return offs[:16].T.reshape(-1).astype(np.int64)


E2M1 = np.array([0.0, 0.5, 1.0, 1.5, 2.0, 3.0, 4.0, 6.0, -0.0, -0.5, -1.0, -1.5, -2.0, -3.0, -4.0, -6.0])


def pack_weight(w, fmt):
    k, n = w.shape
    w = f64(np.asarray(w, np.float32).astype(ml_dtypes.bfloat16)).reshape(k // 32, 32, n)
    amax = np.abs(w).max(1)
    if fmt == "e4m3":
        byte = np.frexp(amax)[1] - 1 + 127 - 7
    else:
        mant, ex = np.frexp(amax / 6.0)
        byte = np.where(mant > 0.5, ex, ex - 1) + 127
    byte = np.clip(np.where(amax > 0, byte, 1), 1, 254)
    scaled = (w * np.exp2(127.0 - byte)[:, None, :]).reshape(k, n).astype(np.float32)
    by_word = np.ascontiguousarray(scaled.reshape(k // 512, 128, 4, n).transpose(0, 1, 3, 2))
    if fmt == "e4m3":
        words = by_word.astype(ml_dtypes.float8_e4m3fn).view(np.uint8)
    else:
        c = by_word.astype(ml_dtypes.float4_e2m1fn).view(np.uint8) & 0xF
        words = (c[..., 0::2] | (c[..., 1::2] << 4)).reshape(k // 512, 128, 2 * n)
    return np.ascontiguousarray(words), np.ascontiguousarray(byte.astype(np.uint8).reshape(k // 512, 16, n))


def unpack_weight(words, scales, fmt):
    g, _, n = scales.shape
    words = np.ascontiguousarray(words).reshape(g, 128, n, -1)
    if fmt == "e4m3":
        vals = words.view(ml_dtypes.float8_e4m3fn).astype(np.float64)
    else:
        nib = np.empty((g, 128, n, 4), np.uint8)
        nib[..., 0::2] = words & 0xF
        nib[..., 1::2] = words >> 4
        vals = E2M1[nib]
    vals = vals * np.repeat(np.exp2(scales.astype(np.float64) - 127.0), 8, axis=1)[..., None]
    return vals.transpose(0, 1, 3, 2).reshape(g * 512, n)


def gelu(v):
    return 0.5 * v * (1.0 + np.tanh(np.sqrt(2.0 / np.pi) * (v + 0.044715 * v**3)))


def often(T, S):
    return np.random.permutation(T)[(T * np.random.uniform(0, 1, S) ** 4).astype(np.int64)]


K, K2, K3, H, T, S, P = 512, 1024, 512, 1024, 2048, 1024, 512

def setup_inputs():
    n = np.random.standard_normal
    s = mx_kscale(K)[:, None]
    s2 = mx_kscale(K2)[:, None]
    s3 = mx_kscale(K3)[:, None]
    u = mx_kscale(H)[:, None]
    d = {}
    d["tab_words"], d["tab_scales"] = pack_weight(n((K, T)) * s, "e4m3")
    d["tab2_words"], d["tab2_scales"] = pack_weight(n((K2, T)) * s2, "e4m3")
    d["tab3_words"], d["tab3_scales"] = pack_weight(n((K3, T)) * s3, "e4m3")
    d["offs"] = striped(np.random.permutation(T)[:S])
    d["offs2"] = striped(np.random.permutation(T)[:S])
    d["offs3"] = striped(np.random.permutation(T)[:S])
    d["pos1"] = striped(np.random.permutation(S)[:P])
    d["pos2"] = striped(often(S, P))
    d["pos3"] = striped(often(S, P))
    d["w1"] = (n((K, H)) / s * u.T / K ** 0.5).astype(np.float32)
    d["w2_words"], d["w2_scales"] = pack_weight(n((K2, H)) / s2 * u.T / K2 ** 0.5, "e2m1")
    d["w3_words"], d["w3_scales"] = pack_weight(n((K3, H)) / s3 * u.T / K3 ** 0.5, "e4m3")
    d["w4"] = (n((H, H)) / u / H ** 0.5).astype(np.float32)
    d["ga"] = (0.8 * np.exp(0.3 * n(H)) / u[:, 0]).astype(np.float32)
    return d

def reference(tab_words, tab_scales, tab2_words, tab2_scales, tab3_words, tab3_scales, offs, offs2, offs3,
              pos1, pos2, pos3, w1, w2_words, w2_scales, w3_words, w3_scales, w4, ga):
    v = unpack_weight(tab_words, tab_scales, "e4m3")[:, unstriped(offs)]
    v2 = unpack_weight(tab2_words, tab2_scales, "e4m3")[:, unstriped(offs2)]
    v3 = unpack_weight(tab3_words, tab3_scales, "e4m3")[:, unstriped(offs3)]
    a = mxq(f64(w1), 0, "e4m3").T @ v
    b = unpack_weight(w2_words, w2_scales, "e2m1").T @ v2
    d = unpack_weight(w3_words, w3_scales, "e4m3").T @ v3
    a1 = a[:, unstriped(pos1)]
    size = np.abs(a1)
    z = np.minimum(size, b[:, unstriped(pos2)]) + np.minimum(size, d[:, unstriped(pos3)])
    y = mxq(f64(w4), 0, "e4m3").T @ mxq(z, 0, "e4m3")
    return y - f64(ga)[:, None] * a1

@@ -1,0 +1,303 @@
+from contextlib import ExitStack
+
+import concourse.mybir as mybir
+from concourse.masks import make_identity
+
+K, K2, K3, H, T, S, J = 512, 1024, 512, 1024, 2048, 1024, 512
+FLOPS = 2 * (K + K2 + K3) * H * S + 2 * H * H * J
+
+F32 = mybir.dt.float32
+BF16 = mybir.dt.bfloat16
+I32 = mybir.dt.int32
+U32 = mybir.dt.uint32
+U16 = mybir.dt.uint16
+U8 = mybir.dt.uint8
+FP8X4 = mybir.dt.float8_e4m3fn_x4
+FP4X4 = mybir.dt.float4_e2m1fn_x4
+ALU = mybir.AluOpType
+ACT = mybir.ActivationFunctionType
+
+P = 128
+BANK = 512
+TILES = H // P
+HALF = J // 2
+LAG = 1
+SPLIT = 7
+RING = 3
+
+
+def tile_list_ballast_treatment_join_kernel(
+    tc, tab_words, tab_scales, tab2_words, tab2_scales, tab3_words, tab3_scales, offs, offs2, offs3,
+    pos1, pos2, pos3, w1, w2_words, w2_scales, w3_words, w3_scales, w4, ga, out,
+):
+    nc = tc.nc
+    with ExitStack() as ctx:
+        keep = ctx.enter_context(tc.tile_pool(name="keep", bufs=1))
+        ring = ctx.enter_context(tc.tile_pool(name="ring", bufs=1))
+        psum = ctx.enter_context(tc.psum_pool(name="psum", bufs=1))
+
+        def held(name, shape, dtype):
+            return keep.tile(shape, dtype, name=name, align_bytes=64)
+
+        def load_list(name, source):
+            tile = keep.tile([P, source.shape[1]], U16, name=name)
+            nc.sync.dma_start(tile[:], source)
+            return tile
+
+        def zeroed(name, shape):
+            tile = held(name, shape, U8)
+            nc.vector.memset(tile[:].bitcast(I32), 0)
+            return tile
+
+        def load_words(words):
+            tile = ring.tile([P, T], I32, name="table", tag="raw", bufs=5, align_bytes=64)
+            nc.sync.dma_start(tile[:], words.rearrange("p t i -> p (t i)").bitcast(I32))
+            return tile
+
+        def load_table_scales(tile, scales):
+            rows = 4 * scales.shape[0]
+            for q in range(4):
+                nc.sync.dma_start(
+                    tile[32 * q : 32 * q + rows, :].bitcast(I32), scales[:, 4 * q : 4 * q + 4, :].bitcast(I32)
+                )
+
+        def load_weight_scales(tile, scales):
+            for q in range(4):
+                nc.sync.dma_start(
+                    tile[32 * q : 32 * q + 4].bitcast(I32),
+                    scales[:, 4 * q : 4 * q + 4, :].rearrange("a r c -> r a c").bitcast(I32),
+                )
+
+        def gather_words(name, table, offsets):
+            tile = held(name, [P, S], U32)
+            nc.vector.tensor_copy(tile[:], table[:].bitcast(U32).indirect(offsets[:]))
+            return tile
+
+        def gather_scales(name, table, offsets):
+            tile = held(name, [P, S], U8)
+            nc.vector.tensor_copy(tile[:], table[:].indirect(offsets[:]))
+            return tile
+
+        def load_weight(rows):
+            tile = ring.tile([P, 4, BANK], F32, name="weight", tag="raw", bufs=5, align_bytes=64)
+            nc.sync.dma_start(tile[:], rows.rearrange("(p t) c -> p t c", t=4))
+            return tile
+
+        def round_weight(raw):
+            tile = ring.tile([P, BANK, 4], BF16, name="rounded", tag="rounded", bufs=4, align_bytes=64)
+            nc.scalar.copy(
+                tile[:].rearrange("p (c i) t -> p c t i", i=4), raw[:].rearrange("p t (c i) -> p c t i", i=4)
+            )
+            return tile
+
+        def quantise(name, rounded):
+            width = rounded.shape[1]
+            codes = held(name + "_codes", [P, width], U32)
+            scales = held(name + "_scales", [P, width], U8)
+            nc.vector.quantize_mx(
+                out=codes[:].bitcast(FP8X4), scales=scales[:], in_=rounded[:].rearrange("p c t -> p (c t)")
+            )
+            return codes, scales
+
+        def scores(passes):
+            tile = ring.tile([P, S], F32, name="scores", tag="scores", bufs=11, align_bytes=64)
+            for m0 in range(0, S, BANK):
+                cols = slice(m0, m0 + BANK)
+                bank = psum.tile([P, BANK], F32, name="product", tag="product", bufs=4)
+                for a, (w_codes, w_scales, v_codes, v_scales) in enumerate(passes):
+                    nc.tensor.matmul_mx(
+                        out=bank[:], lhsT=w_codes, lhsT_scale=w_scales,
+                        rhs=v_codes[:, cols].bitcast(FP8X4), rhs_scale=v_scales[:, cols],
+                        start=(a == 0), stop=(a == len(passes) - 1),
+                    )
+                nc.scalar.copy(tile[:, cols], bank[:])
+            return tile
+
+        tab_plane = zeroed("tab_plane", [P, T])
+        tab3_plane = zeroed("tab3_plane", [P, T])
+        tab2_plane = zeroed("tab2_plane", [P, T])
+        w3_plane = zeroed("w3_plane", [P, 1, H])
+        w2_plane = zeroed("w2_plane", [P, 2, H])
+        v2_scales_1 = zeroed("v2_scales_1", [P, S])
+        identity = held("identity", [P, P], F32)
+        make_identity(nc, identity[:])
+
+        offs_t = load_list("offs", offs)
+        offs3_t = load_list("offs3", offs3)
+        offs2_t = load_list("offs2", offs2)
+        pos1_t = load_list("pos1", pos1)
+        pos3_t = load_list("pos3", pos3)
+        tab_t = load_words(tab_words[0])
+        pos2_t = load_list("pos2", pos2)
+        ga_t = held("ga", [P, TILES], F32)
+        with nc.allow_non_contiguous_dma(reason="one gain to a partition"):
+            nc.sync.dma_start(ga_t[:], ga.rearrange("(c p) -> p c", p=P))
+        load_table_scales(tab_plane, tab_scales)
+        w1_raw = [load_weight(w1[:, 0:BANK])]
+        w1_raw.append(load_weight(w1[:, BANK:H]))
+        load_table_scales(tab3_plane, tab3_scales)
+        tab3_t = load_words(tab3_words[0])
+        load_table_scales(tab2_plane, tab2_scales)
+        tab2_t = [load_words(tab2_words[0])]
+        w3_t = held("w3", [P, H], I32)
+        nc.sync.dma_start(w3_t[:], w3_words[0].rearrange("p c i -> p (c i)").bitcast(I32))
+        load_weight_scales(w3_plane, w3_scales)
+        tab2_t.append(load_words(tab2_words[1]))
+        w2_t = held("w2", [P, 2, 2 * H], U8)
+        nc.sync.dma_start(w2_t[:].bitcast(I32), w2_words.rearrange("a p c -> p a c").bitcast(I32))
+        load_weight_scales(w2_plane, w2_scales)
+
+        v_codes = gather_words("v_codes", tab_t, offs_t)
+        v_scales = gather_scales("v_scales", tab_plane, offs_t)
+        minus_ga = held("minus_ga", [P, TILES], F32)
+        nc.scalar.mul(minus_ga[:], ga_t[:], -1.0)
+        w1_q = [quantise("w1_%d" % h, round_weight(w1_raw[h])) for h in range(2)]
+        v3_scales = gather_scales("v3_scales", tab3_plane, offs3_t)
+        v3_codes = gather_words("v3_codes", tab3_t, offs3_t)
+        v2_scales = gather_scales("v2_scales", tab2_plane, offs2_t)
+        for r in range(4):
+            nc.sync.dma_start(v2_scales_1[r:P:32, :].bitcast(I32), v2_scales[4 + r : P : 32, :].bitcast(I32))
+        v2_codes = [gather_words("v2_codes_%d" % a, tab2_t[a], offs2_t) for a in range(2)]
+        w4_raw = [
+            load_weight(w4[b * BANK : (b + 1) * BANK, g * BANK : (g + 1) * BANK]) for g in range(2) for b in range(2)
+        ]
+
+        picked_a = []
+        for c in range(TILES):
+            codes, scales = w1_q[c // 4]
+            cols = slice(P * (c % 4), P * (c % 4 + 1))
+            a_t = scores([(codes[:, cols].bitcast(FP8X4), scales[:, cols], v_codes, v_scales)])
+            picked = held("picked_a_%d" % c, [P, J], F32)
+            nc.vector.tensor_copy(picked[:], a_t[:].indirect(pos1_t[:]))
+            picked_a.append(picked)
+
+        capped_d = []
+        w4_rounded = []
+        for c in range(TILES):
+            cols = slice(P * c, P * (c + 1))
+            d_t = scores([(w3_t[:, cols].bitcast(FP8X4), w3_plane[:, 0, cols], v3_codes, v3_scales)])
+            capped = held("capped_d_%d" % c, [P, J], F32)
+            nc.vector.tensor_copy(capped[:], d_t[:].indirect(pos3_t[:]))
+            capped_d.append(capped)
+            if c % 2 == 1:
+                w4_rounded.append(round_weight(w4_raw[c // 2]))
+
+        def b_scores(c):
+            return scores(
+                [
+                    (
+                        w2_t[:, a, 2 * P * c : 2 * P * (c + 1)].bitcast(FP4X4),
+                        w2_plane[:, a, P * c : P * (c + 1)],
+                        v2_codes[a],
+                        (v2_scales, v2_scales_1)[a],
+                    )
+                    for a in range(2)
+                ]
+            )
+
+        capped_b = [held("capped_b_%d" % i, [P, J], F32) for i in range(RING)]
+        size = {}
+        z_rows = [held("z_rows_%d" % b, [P, 4, BANK], BF16) for b in range(2)]
+        z_q = {}
+
+        def pick_b(unit, b_t, j0, j1):
+            nc.vector.tensor_copy(
+                capped_b[unit % RING][:, 0 : j1 - j0], b_t[:].indirect(pos2_t[:, j0 // 16 : j1 // 16])
+            )
+
+        def cap_d(c):
+            size[c] = keep.tile([P, J], F32, name="size", tag="size_%d" % c, align_bytes=64)
+            nc.scalar.activation(size[c][:], picked_a[c][:], ACT.Abs)
+            nc.vector.tensor_tensor(capped_d[c][:], capped_d[c][:], size[c][:], ALU.min)
+
+        def join(unit, c, j0, j1):
+            capped = capped_b[unit % RING]
+            width = j1 - j0
+            nc.vector.tensor_tensor(capped[:, 0:width], capped[:, 0:width], size[c][:, j0:j1], ALU.min)
+            bank = psum.tile([P, 4, P], F32, name="z_sum", tag="z_sum", bufs=2)
+            for i in range(width // P):
+                for first, term in (
+                    (True, capped[:, P * i : P * (i + 1)]),
+                    (False, capped_d[c][:, j0 + P * i : j0 + P * (i + 1)]),
+                ):
+                    nc.tensor.matmul(
+                        bank[:, i, :], lhsT=term, rhs=identity[:], is_transpose=True, start=first, stop=not first
+                    )
+            return bank
+
+        def z_out(c, bank, j0, j1):
+            blocks = (j1 - j0) // P
+            nc.scalar.copy(
+                z_rows[c // 4][:, j0 // P : j1 // P, P * (c % 4) : P * (c % 4 + 1)], bank[:, 0:blocks, :]
+            )
+
+        def z_turn(b, h):
+            rows = z_rows[b]
+            i0 = 2 * h
+            bank = psum.tile([P, 2, 2, P], F32, name="z_words", tag="z_words", bufs=2)
+            for i in range(2):
+                words = rows[:, i0 + i, :].bitcast(F32)
+                for u in range(2):
+                    nc.tensor.transpose(bank[:, i, u, :], words[:, u : 2 * P : 2], identity[:])
+            grouped = held("z_grouped_%d_%d" % (b, h), [P, HALF, 4], BF16)
+            nc.scalar.copy(
+                grouped[:].bitcast(F32).rearrange("p (i j) u -> p i j u", i=2),
+                bank[:].rearrange("p i u j -> p i j u"),
+            )
+            z_q[b, h] = quantise("z_%d_%d" % (b, h), grouped)
+
+        def finish(h, w4_q):
+            j_cols = slice(HALF * h, HALF * (h + 1))
+            for c0 in range(0, TILES, 2):
+                bank = psum.tile([P, 2, HALF], F32, name="product", tag="product", bufs=4)
+                staged = ring.tile([P, 2, HALF], F32, name="staged", tag="staged", bufs=4, align_bytes=64)
+                for i in range(2):
+                    c = c0 + i
+                    cols = slice(P * (c % 4), P * (c % 4 + 1))
+                    for b in (1, 0):
+                        codes, scales = w4_q[2 * (c // 4) + b]
+                        nc.tensor.matmul_mx(
+                            out=bank[:, i, :], lhsT=codes[:, cols].bitcast(FP8X4), lhsT_scale=scales[:, cols],
+                            rhs=z_q[b, h][0][:].bitcast(FP8X4), rhs_scale=z_q[b, h][1][:],
+                            start=(b == 1), stop=(b == 0),
+                        )
+                for i in range(2):
+                    c = c0 + i
+                    nc.vector.scalar_tensor_tensor(
+                        staged[:, i, :], picked_a[c][:, j_cols], minus_ga[:, c : c + 1], bank[:, i, :],
+                        ALU.mult, ALU.add,
+                    )
+                nc.sync.dma_start(out.rearrange("(c p) j -> p c j", p=P)[:, c0 : c0 + 2, j_cols], staged[:])
+
+        units = [(c, 0, J) for c in range(SPLIT)]
+        units = units + [(c, 0, HALF) for c in range(SPLIT, TILES)] + [(c, HALF, J) for c in range(SPLIT, TILES)]
+        b_t, banks = [], {}
+        for step in range(len(units) + LAG + 1):
+            if step < TILES:
+                b_t.append(b_scores(step))
+            if step < len(units):
+                c, j0, j1 = units[step]
+                pick_b(step, b_t[c], j0, j1)
+            if 1 <= step <= TILES:
+                cap_d(step - 1)
+            if 1 <= step <= len(units):
+                c, j0, j1 = units[step - 1]
+                banks[step - 1] = join(step - 1, c, j0, j1)
+            done = step - 1 - LAG
+            if done >= 0:
+                c, j0, j1 = units[done]
+                z_out(c, banks[done], j0, j1)
+                if c % 4 == 3:
+                    for h in range(j0 // HALF, j1 // HALF):
+                        z_turn(c // 4, h)
+        w4_planes = keep.tile([P, BANK], U8, name="w4_planes", tag="size_%d" % (TILES - 1), align_bytes=64)
+        w4_q = []
+        for i in range(4):
+            codes = held("w4_codes_%d" % i, [P, BANK], U32)
+            nc.vector.quantize_mx(
+                out=codes[:].bitcast(FP8X4), scales=w4_planes[4 * i : P, :],
+                in_=w4_rounded[i][:].rearrange("p c t -> p (c t)"),
+            )
+            w4_q.append((codes, w4_planes[4 * i : P, :]))
+        finish(0, w4_q)
+        finish(1, w4_q)

@@ -21,6 +21,7 @@ P = 128
 BANK = 512
 TILES = H // P
 HALF = J // 2
+SZ = 1
 LAG = 1
 SPLIT = 7
 RING = 3
@@ -49,23 +50,21 @@ def tile_list_ballast_treatment_join_kernel(
             nc.vector.memset(tile[:].bitcast(I32), 0)
             return tile
 
-        def load_words(words):
-            tile = ring.tile([P, T], I32, name="table", tag="raw", bufs=5, align_bytes=64)
+        def load_words(words, slot):
+            tile = ring.tile([P, T], I32, name="table", tag="slot_%d" % slot, align_bytes=64)
             nc.sync.dma_start(tile[:], words.rearrange("p t i -> p (t i)").bitcast(I32))
             return tile
 
-        def load_table_scales(tile, scales):
-            rows = 4 * scales.shape[0]
-            for q in range(4):
+        def load_scales(tile, scales):
+            for r in range(4):
                 nc.sync.dma_start(
-                    tile[32 * q : 32 * q + rows, :].bitcast(I32), scales[:, 4 * q : 4 * q + 4, :].bitcast(I32)
+                    tile[r:P:32].bitcast(I32), scales[:, r:16:4, :].rearrange("a q c -> q a c").bitcast(I32)
                 )
 
-        def load_weight_scales(tile, scales):
+        def load_stacked_scales(tile, scales):
             for q in range(4):
                 nc.sync.dma_start(
-                    tile[32 * q : 32 * q + 4].bitcast(I32),
-                    scales[:, 4 * q : 4 * q + 4, :].rearrange("a r c -> r a c").bitcast(I32),
+                    tile[32 * q : 32 * q + 8, :].bitcast(I32), scales[:, 4 * q : 4 * q + 4, :].bitcast(I32)
                 )
 
         def gather_words(name, table, offsets):
@@ -75,19 +74,21 @@ def tile_list_ballast_treatment_join_kernel(
 
         def gather_scales(name, table, offsets):
             tile = held(name, [P, S], U8)
-            nc.vector.tensor_copy(tile[:], table[:].indirect(offsets[:]))
+            nc.vector.tensor_copy(tile[:], table.indirect(offsets[:]))
             return tile
 
-        def load_weight(rows):
-            tile = ring.tile([P, 4, BANK], F32, name="weight", tag="raw", bufs=5, align_bytes=64)
+        def load_weight(rows, slot):
+            tile = ring.tile([P, 4, BANK], F32, name="weight", tag="slot_%d" % slot, align_bytes=64)
             nc.sync.dma_start(tile[:], rows.rearrange("(p t) c -> p t c", t=4))
             return tile
 
-        def round_weight(raw):
-            tile = ring.tile([P, BANK, 4], BF16, name="rounded", tag="rounded", bufs=4, align_bytes=64)
-            nc.scalar.copy(
-                tile[:].rearrange("p (c i) t -> p c t i", i=4), raw[:].rearrange("p t (c i) -> p c t i", i=4)
-            )
+        def round_weights(halves):
+            tile = ring.tile([P, H, 4], BF16, name="rounded", tag="rounded", bufs=2, align_bytes=64)
+            for i, raw in enumerate(halves):
+                nc.scalar.copy(
+                    tile[:, BANK * i : BANK * (i + 1), :].rearrange("p (c i) t -> p c t i", i=4),
+                    raw[:].rearrange("p t (c i) -> p c t i", i=4),
+                )
             return tile
 
         def quantise(name, rounded):
@@ -100,10 +101,10 @@ def tile_list_ballast_treatment_join_kernel(
             return codes, scales
 
         def scores(passes):
-            tile = ring.tile([P, S], F32, name="scores", tag="scores", bufs=11, align_bytes=64)
+            tile = ring.tile([P, S], F32, name="scores", tag="scores", bufs=16, align_bytes=64)
             for m0 in range(0, S, BANK):
                 cols = slice(m0, m0 + BANK)
-                bank = psum.tile([P, BANK], F32, name="product", tag="product", bufs=4)
+                bank = psum.tile([P, BANK], F32, name="product", tag="product", bufs=6)
                 for a, (w_codes, w_scales, v_codes, v_scales) in enumerate(passes):
                     nc.tensor.matmul_mx(
                         out=bank[:], lhsT=w_codes, lhsT_scale=w_scales,
@@ -113,60 +114,63 @@ def tile_list_ballast_treatment_join_kernel(
                 nc.scalar.copy(tile[:, cols], bank[:])
             return tile
 
-        tab_plane = zeroed("tab_plane", [P, T])
-        tab3_plane = zeroed("tab3_plane", [P, T])
+        tab_plane = zeroed("tab_plane", [P, 1, T])
+        tab3_plane = zeroed("tab3_plane", [P, 1, T])
         tab2_plane = zeroed("tab2_plane", [P, T])
         w3_plane = zeroed("w3_plane", [P, 1, H])
         w2_plane = zeroed("w2_plane", [P, 2, H])
         v2_scales_1 = zeroed("v2_scales_1", [P, S])
         identity = held("identity", [P, P], F32)
+        ga_rows = held("ga_rows", [P, P], F32)
+        nc.gpsimd.memset(ga_rows[:], 0.0)
         make_identity(nc, identity[:])
+
+        def load_w4(i):
+            g, b = divmod(i, 2)
+            return load_weight(w4[b * BANK : (b + 1) * BANK, g * BANK : (g + 1) * BANK], i)
 
         offs_t = load_list("offs", offs)
         offs3_t = load_list("offs3", offs3)
+        tab_t = load_words(tab_words[0], 0)
         offs2_t = load_list("offs2", offs2)
-        pos1_t = load_list("pos1", pos1)
-        pos3_t = load_list("pos3", pos3)
-        tab_t = load_words(tab_words[0])
-        pos2_t = load_list("pos2", pos2)
-        ga_t = held("ga", [P, TILES], F32)
-        with nc.allow_non_contiguous_dma(reason="one gain to a partition"):
-            nc.sync.dma_start(ga_t[:], ga.rearrange("(c p) -> p c", p=P))
-        load_table_scales(tab_plane, tab_scales)
-        w1_raw = [load_weight(w1[:, 0:BANK])]
-        w1_raw.append(load_weight(w1[:, BANK:H]))
-        load_table_scales(tab3_plane, tab3_scales)
-        tab3_t = load_words(tab3_words[0])
-        load_table_scales(tab2_plane, tab2_scales)
-        tab2_t = [load_words(tab2_words[0])]
+        nc.sync.dma_start(ga_rows[0:TILES, :], ga.rearrange("(c p) -> c p", p=P))
+        load_scales(tab_plane, tab_scales)
+        w1_raw = [load_weight(w1[:, 0:BANK], 1)]
+        load_scales(tab3_plane, tab3_scales)
+        w1_raw.append(load_weight(w1[:, BANK:H], 2))
+        tab3_t = load_words(tab3_words[0], 3)
         w3_t = held("w3", [P, H], I32)
         nc.sync.dma_start(w3_t[:], w3_words[0].rearrange("p c i -> p (c i)").bitcast(I32))
-        load_weight_scales(w3_plane, w3_scales)
-        tab2_t.append(load_words(tab2_words[1]))
-        w2_t = held("w2", [P, 2, 2 * H], U8)
-        nc.sync.dma_start(w2_t[:].bitcast(I32), w2_words.rearrange("a p c -> p a c").bitcast(I32))
-        load_weight_scales(w2_plane, w2_scales)
+        load_scales(w3_plane, w3_scales)
+        load_stacked_scales(tab2_plane, tab2_scales)
+        tab2_t = [load_words(tab2_words[a], 4 + a) for a in range(2)]
+        pos1_t = load_list("pos1", pos1)
+        pos3_t = load_list("pos3", pos3)
+        pos2_t = load_list("pos2", pos2)
 
         v_codes = gather_words("v_codes", tab_t, offs_t)
-        v_scales = gather_scales("v_scales", tab_plane, offs_t)
+        v_scales = gather_scales("v_scales", tab_plane[:, 0, :], offs_t)
         minus_ga = held("minus_ga", [P, TILES], F32)
-        nc.scalar.mul(minus_ga[:], ga_t[:], -1.0)
-        w1_q = [quantise("w1_%d" % h, round_weight(w1_raw[h])) for h in range(2)]
-        v3_scales = gather_scales("v3_scales", tab3_plane, offs3_t)
+        ga_bank = psum.tile([P, P], F32, name="ga_bank", tag="turn_0")
+        nc.tensor.transpose(ga_bank[:], ga_rows[:], identity[:])
+        nc.scalar.mul(minus_ga[:], ga_bank[:, 0:TILES], -1.0)
+        w1_codes, w1_scales = quantise("w1", round_weights(w1_raw))
+        v3_scales = gather_scales("v3_scales", tab3_plane[:, 0, :], offs3_t)
         v3_codes = gather_words("v3_codes", tab3_t, offs3_t)
-        v2_scales = gather_scales("v2_scales", tab2_plane, offs2_t)
+        v2_scales = gather_scales("v2_scales", tab2_plane[:], offs2_t)
+        w4_raw = [load_w4(0)]
+        w2_t = held("w2", [P, 2, 2 * H], U8)
+        nc.sync.dma_start(w2_t[:].bitcast(I32), w2_words.rearrange("a p c -> p a c").bitcast(I32))
+        load_scales(w2_plane, w2_scales)
         for r in range(4):
             nc.sync.dma_start(v2_scales_1[r:P:32, :].bitcast(I32), v2_scales[4 + r : P : 32, :].bitcast(I32))
+        w4_raw.extend(load_w4(i) for i in range(1, 4))
         v2_codes = [gather_words("v2_codes_%d" % a, tab2_t[a], offs2_t) for a in range(2)]
-        w4_raw = [
-            load_weight(w4[b * BANK : (b + 1) * BANK, g * BANK : (g + 1) * BANK]) for g in range(2) for b in range(2)
-        ]
 
         picked_a = []
         for c in range(TILES):
-            codes, scales = w1_q[c // 4]
-            cols = slice(P * (c % 4), P * (c % 4 + 1))
-            a_t = scores([(codes[:, cols].bitcast(FP8X4), scales[:, cols], v_codes, v_scales)])
+            cols = slice(P * c, P * (c + 1))
+            a_t = scores([(w1_codes[:, cols].bitcast(FP8X4), w1_scales[:, cols], v_codes, v_scales)])
             picked = held("picked_a_%d" % c, [P, J], F32)
             nc.vector.tensor_copy(picked[:], a_t[:].indirect(pos1_t[:]))
             picked_a.append(picked)
@@ -179,8 +183,7 @@ def tile_list_ballast_treatment_join_kernel(
             capped = held("capped_d_%d" % c, [P, J], F32)
             nc.vector.tensor_copy(capped[:], d_t[:].indirect(pos3_t[:]))
             capped_d.append(capped)
-            if c % 2 == 1:
-                w4_rounded.append(round_weight(w4_raw[c // 2]))
+        w4_rounded.extend(round_weights(w4_raw[2 * g : 2 * g + 2]) for g in range(2))
 
         def b_scores(c):
             return scores(
@@ -195,26 +198,33 @@ def tile_list_ballast_treatment_join_kernel(
                 ]
             )
 
-        capped_b = [held("capped_b_%d" % i, [P, J], F32) for i in range(RING)]
+        capped_b4 = [
+            ring.tile([P, 4, J], F32, name="capped_b", tag="slot_%d" % (4 + i), align_bytes=64) for i in range(2)
+        ]
+        size4 = [ring.tile([P, 4, J], F32, name="size", tag="slot_%d" % (SZ + i), align_bytes=64) for i in range(2)]
+        capped_b = [capped_b4[c // 4][:, c % 4, :] for c in range(TILES)]
         size = {}
         z_rows = [held("z_rows_%d" % b, [P, 4, BANK], BF16) for b in range(2)]
         z_q = {}
 
-        def pick_b(unit, b_t, j0, j1):
-            nc.vector.tensor_copy(
-                capped_b[unit % RING][:, 0 : j1 - j0], b_t[:].indirect(pos2_t[:, j0 // 16 : j1 // 16])
-            )
+        def pick_b(c, b_t, j0, j1):
+            nc.vector.tensor_copy(capped_b[c][:, j0:j1], b_t[:].indirect(pos2_t[:, j0 // 16 : j1 // 16]))
 
         def cap_d(c):
-            size[c] = keep.tile([P, J], F32, name="size", tag="size_%d" % c, align_bytes=64)
+            size[c] = size4[c // 4][:, c % 4, :]
             nc.scalar.activation(size[c][:], picked_a[c][:], ACT.Abs)
             nc.vector.tensor_tensor(capped_d[c][:], capped_d[c][:], size[c][:], ALU.min)
 
-        def join(unit, c, j0, j1):
-            capped = capped_b[unit % RING]
+        def cap_b(c, j0, j1):
+            nc.vector.tensor_tensor(capped_b[c][:, j0:j1], capped_b[c][:, j0:j1], size[c][:, j0:j1], ALU.min)
+
+        def join(c, j0, j1, turn):
             width = j1 - j0
-            nc.vector.tensor_tensor(capped[:, 0:width], capped[:, 0:width], size[c][:, j0:j1], ALU.min)
-            bank = psum.tile([P, 4, P], F32, name="z_sum", tag="z_sum", bufs=2)
+            capped = capped_b[c][:, j0:j1]
+            if c < 6:
+                bank = psum.tile([P, 4, P], F32, name="z_sum", tag="product", bufs=6)
+            else:
+                bank = psum.tile([P, 4, P], F32, name="z_sum", tag="turn_%d" % turn)
             for i in range(width // P):
                 for first, term in (
                     (True, capped[:, P * i : P * (i + 1)]),
@@ -234,7 +244,7 @@ def tile_list_ballast_treatment_join_kernel(
         def z_turn(b, h):
             rows = z_rows[b]
             i0 = 2 * h
-            bank = psum.tile([P, 2, 2, P], F32, name="z_words", tag="z_words", bufs=2)
+            bank = psum.tile([P, 2, 2, P], F32, name="z_words", tag="turn_%d" % ((b + h) % 2))
             for i in range(2):
                 words = rows[:, i0 + i, :].bitcast(F32)
                 for u in range(2):
@@ -248,9 +258,10 @@ def tile_list_ballast_treatment_join_kernel(
 
         def finish(h, w4_q):
             j_cols = slice(HALF * h, HALF * (h + 1))
+            staged4 = ring.tile([P, 4, 2, HALF], F32, name="staged", tag="slot_%d" % (3 * h), align_bytes=64)
             for c0 in range(0, TILES, 2):
-                bank = psum.tile([P, 2, HALF], F32, name="product", tag="product", bufs=4)
-                staged = ring.tile([P, 2, HALF], F32, name="staged", tag="staged", bufs=4, align_bytes=64)
+                bank = psum.tile([P, 2, HALF], F32, name="product", tag="product", bufs=6)
+                staged = staged4[:, c0 // 2, :, :]
                 for i in range(2):
                     c = c0 + i
                     cols = slice(P * (c % 4), P * (c % 4 + 1))
@@ -267,37 +278,32 @@ def tile_list_ballast_treatment_join_kernel(
                         staged[:, i, :], picked_a[c][:, j_cols], minus_ga[:, c : c + 1], bank[:, i, :],
                         ALU.mult, ALU.add,
                     )
-                nc.sync.dma_start(out.rearrange("(c p) j -> p c j", p=P)[:, c0 : c0 + 2, j_cols], staged[:])
+                nc.sync.dma_start(out.rearrange("(c p) j -> p c j", p=P)[:, c0 : c0 + 2, j_cols], staged)
 
-        units = [(c, 0, J) for c in range(SPLIT)]
-        units = units + [(c, 0, HALF) for c in range(SPLIT, TILES)] + [(c, HALF, J) for c in range(SPLIT, TILES)]
-        b_t, banks = [], {}
-        for step in range(len(units) + LAG + 1):
-            if step < TILES:
-                b_t.append(b_scores(step))
-            if step < len(units):
-                c, j0, j1 = units[step]
-                pick_b(step, b_t[c], j0, j1)
-            if 1 <= step <= TILES:
-                cap_d(step - 1)
-            if 1 <= step <= len(units):
-                c, j0, j1 = units[step - 1]
-                banks[step - 1] = join(step - 1, c, j0, j1)
-            done = step - 1 - LAG
-            if done >= 0:
-                c, j0, j1 = units[done]
-                z_out(c, banks[done], j0, j1)
-                if c % 4 == 3:
-                    for h in range(j0 // HALF, j1 // HALF):
-                        z_turn(c // 4, h)
-        w4_planes = keep.tile([P, BANK], U8, name="w4_planes", tag="size_%d" % (TILES - 1), align_bytes=64)
+        for c in range(TILES + 1):
+            if c < TILES:
+                pick_b(c, b_scores(c), 0, J)
+            if c >= 1:
+                cap_d(c - 1)
+                cap_b(c - 1, 0, J)
+        for c in range(TILES - 1):
+            z_out(c, join(c, 0, J, c % 2), 0, J)
+            if c == 3:
+                for h in range(2):
+                    z_turn(0, h)
+        for h in range(2):
+            z_out(TILES - 1, join(TILES - 1, HALF * h, HALF * (h + 1), 1 - h), HALF * h, HALF * (h + 1))
+        for h in range(2):
+            z_turn(1, h)
+        w4_planes = ring.tile([P, 2, H], U8, name="w4_planes", tag="slot_%d" % (SZ + 1), align_bytes=64)
         w4_q = []
-        for i in range(4):
-            codes = held("w4_codes_%d" % i, [P, BANK], U32)
+        for g in range(2):
+            codes = held("w4_codes_%d" % g, [P, H], U32)
             nc.vector.quantize_mx(
-                out=codes[:].bitcast(FP8X4), scales=w4_planes[4 * i : P, :],
-                in_=w4_rounded[i][:].rearrange("p c t -> p (c t)"),
+                out=codes[:].bitcast(FP8X4), scales=w4_planes[:, g, :],
+                in_=w4_rounded[g][:].rearrange("p c t -> p (c t)"),
             )
-            w4_q.append((codes, w4_planes[4 * i : P, :]))
+            for b in range(2):
+                w4_q.append((codes[:, BANK * b : BANK * (b + 1)], w4_planes[:, g, BANK * b : BANK * (b + 1)]))
         finish(0, w4_q)
         finish(1, w4_q)

@@ -21,10 +21,6 @@ P = 128
 BANK = 512
 TILES = H // P
 HALF = J // 2
-SZ = 1
-LAG = 1
-SPLIT = 7
-RING = 3
 
 
 def tile_list_ballast_treatment_join_kernel(
@@ -45,8 +41,8 @@ def tile_list_ballast_treatment_join_kernel(
             nc.sync.dma_start(tile[:], source)
             return tile
 
-        def zeroed(name, shape):
-            tile = held(name, shape, U8)
+        def zeroed(name, shape, tag=None):
+            tile = ring.tile(shape, U8, name=name, tag=tag or name, align_bytes=64)
             nc.vector.memset(tile[:].bitcast(I32), 0)
             return tile
 
@@ -55,8 +51,8 @@ def tile_list_ballast_treatment_join_kernel(
             nc.sync.dma_start(tile[:], words.rearrange("p t i -> p (t i)").bitcast(I32))
             return tile
 
-        def load_scales(tile, scales):
-            for r in range(4):
+        def load_scales(tile, scales, rows=range(4)):
+            for r in rows:
                 nc.sync.dma_start(
                     tile[r:P:32].bitcast(I32), scales[:, r:16:4, :].rearrange("a q c -> q a c").bitcast(I32)
                 )
@@ -82,23 +78,11 @@ def tile_list_ballast_treatment_join_kernel(
             nc.sync.dma_start(tile[:], rows.rearrange("(p t) c -> p t c", t=4))
             return tile
 
-        def round_weights(halves):
-            tile = ring.tile([P, H, 4], BF16, name="rounded", tag="rounded", bufs=2, align_bytes=64)
-            for i, raw in enumerate(halves):
-                nc.scalar.copy(
-                    tile[:, BANK * i : BANK * (i + 1), :].rearrange("p (c i) t -> p c t i", i=4),
-                    raw[:].rearrange("p t (c i) -> p c t i", i=4),
-                )
-            return tile
+        def round_weight(copy, rounded, raw):
+            copy(rounded.rearrange("p (c i) t -> p c t i", i=4), raw[:].rearrange("p t (c i) -> p c t i", i=4))
 
-        def quantise(name, rounded):
-            width = rounded.shape[1]
-            codes = held(name + "_codes", [P, width], U32)
-            scales = held(name + "_scales", [P, width], U8)
-            nc.vector.quantize_mx(
-                out=codes[:].bitcast(FP8X4), scales=scales[:], in_=rounded[:].rearrange("p c t -> p (c t)")
-            )
-            return codes, scales
+        def quantise(codes, scales, rounded):
+            nc.vector.quantize_mx(out=codes.bitcast(FP8X4), scales=scales, in_=rounded.rearrange("p c t -> p (c t)"))
 
         def scores(passes):
             tile = ring.tile([P, S], F32, name="scores", tag="scores", bufs=16, align_bytes=64)
@@ -114,11 +98,11 @@ def tile_list_ballast_treatment_join_kernel(
                 nc.scalar.copy(tile[:, cols], bank[:])
             return tile
 
-        tab_plane = zeroed("tab_plane", [P, 1, T])
         tab3_plane = zeroed("tab3_plane", [P, 1, T])
+        tab_plane = zeroed("tab_plane", [P, 1, T])
         tab2_plane = zeroed("tab2_plane", [P, T])
         w3_plane = zeroed("w3_plane", [P, 1, H])
-        w2_plane = zeroed("w2_plane", [P, 2, H])
+        w2_plane = zeroed("w2_plane", [P, 2, H], "last_1")
         v2_scales_1 = zeroed("v2_scales_1", [P, S])
         identity = held("identity", [P, P], F32)
         ga_rows = held("ga_rows", [P, P], F32)
@@ -134,32 +118,39 @@ def tile_list_ballast_treatment_join_kernel(
         tab_t = load_words(tab_words[0], 0)
         offs2_t = load_list("offs2", offs2)
         nc.sync.dma_start(ga_rows[0:TILES, :], ga.rearrange("(c p) -> c p", p=P))
-        load_scales(tab_plane, tab_scales)
-        w1_raw = [load_weight(w1[:, 0:BANK], 1)]
         load_scales(tab3_plane, tab3_scales)
+        w1_raw = [load_weight(w1[:, 0:BANK], 1)]
+        load_scales(tab_plane, tab_scales, range(3))
         w1_raw.append(load_weight(w1[:, BANK:H], 2))
+        load_scales(tab_plane, tab_scales, range(3, 4))
         tab3_t = load_words(tab3_words[0], 3)
-        w3_t = held("w3", [P, H], I32)
-        nc.sync.dma_start(w3_t[:], w3_words[0].rearrange("p c i -> p (c i)").bitcast(I32))
-        load_scales(w3_plane, w3_scales)
         load_stacked_scales(tab2_plane, tab2_scales)
         tab2_t = [load_words(tab2_words[a], 4 + a) for a in range(2)]
         pos1_t = load_list("pos1", pos1)
+        w3_t = held("w3", [P, H], I32)
+        nc.sync.dma_start(w3_t[:], w3_words[0].rearrange("p c i -> p (c i)").bitcast(I32))
+        load_scales(w3_plane, w3_scales)
         pos3_t = load_list("pos3", pos3)
         pos2_t = load_list("pos2", pos2)
 
         v_codes = gather_words("v_codes", tab_t, offs_t)
-        v_scales = gather_scales("v_scales", tab_plane[:, 0, :], offs_t)
+        v3_scales = gather_scales("v3_scales", tab3_plane[:, 0, :], offs3_t)
         minus_ga = held("minus_ga", [P, TILES], F32)
         ga_bank = psum.tile([P, P], F32, name="ga_bank", tag="turn_0")
         nc.tensor.transpose(ga_bank[:], ga_rows[:], identity[:])
         nc.scalar.mul(minus_ga[:], ga_bank[:, 0:TILES], -1.0)
-        w1_codes, w1_scales = quantise("w1", round_weights(w1_raw))
-        v3_scales = gather_scales("v3_scales", tab3_plane[:, 0, :], offs3_t)
+        w1_rounded = ring.tile([P, H, 4], BF16, name="w1_rounded", tag="rounded", align_bytes=64)
+        w1_codes = held("w1_codes", [P, H], U32)
+        w1_scales = held("w1_scales", [P, H], U8)
+        for g in range(2):
+            cols = slice(BANK * g, BANK * (g + 1))
+            round_weight(nc.scalar.copy, w1_rounded[:, cols, :], w1_raw[g])
+            quantise(w1_codes[:, cols], w1_scales[:, cols], w1_rounded[:, cols, :])
+        v_scales = gather_scales("v_scales", tab_plane[:, 0, :], offs_t)
         v3_codes = gather_words("v3_codes", tab3_t, offs3_t)
         v2_scales = gather_scales("v2_scales", tab2_plane[:], offs2_t)
         w4_raw = [load_w4(0)]
-        w2_t = held("w2", [P, 2, 2 * H], U8)
+        w2_t = ring.tile([P, 2, 2 * H], U8, name="w2", tag="last_0", align_bytes=64)
         nc.sync.dma_start(w2_t[:].bitcast(I32), w2_words.rearrange("a p c -> p a c").bitcast(I32))
         load_scales(w2_plane, w2_scales)
         for r in range(4):
@@ -176,14 +167,17 @@ def tile_list_ballast_treatment_join_kernel(
             picked_a.append(picked)
 
         capped_d = []
-        w4_rounded = []
         for c in range(TILES):
             cols = slice(P * c, P * (c + 1))
             d_t = scores([(w3_t[:, cols].bitcast(FP8X4), w3_plane[:, 0, cols], v3_codes, v3_scales)])
             capped = held("capped_d_%d" % c, [P, J], F32)
             nc.vector.tensor_copy(capped[:], d_t[:].indirect(pos3_t[:]))
             capped_d.append(capped)
-        w4_rounded.extend(round_weights(w4_raw[2 * g : 2 * g + 2]) for g in range(2))
+        w4_low = ring.tile([P, H, 4], BF16, name="w4_low", tag="rounded", align_bytes=64)
+        w4_high = [held("w4_high_0", [P, BANK, 4], BF16)]
+        round_weight(nc.scalar.copy, w4_low[:, 0:BANK, :], w4_raw[0])
+        round_weight(nc.scalar.copy, w4_low[:, BANK:H, :], w4_raw[1])
+        round_weight(nc.scalar.copy, w4_high[0][:], w4_raw[2])
 
         def b_scores(c):
             return scores(
@@ -201,30 +195,23 @@ def tile_list_ballast_treatment_join_kernel(
         capped_b4 = [
             ring.tile([P, 4, J], F32, name="capped_b", tag="slot_%d" % (4 + i), align_bytes=64) for i in range(2)
         ]
-        size4 = [ring.tile([P, 4, J], F32, name="size", tag="slot_%d" % (SZ + i), align_bytes=64) for i in range(2)]
+        size4 = [ring.tile([P, 4, J], F32, name="size", tag="slot_%d" % (1 + i), align_bytes=64) for i in range(2)]
+        last_size = [
+            ring.tile([P, HALF], F32, name="last_size", tag="last_%d" % h, align_bytes=64) for h in range(2)
+        ]
         capped_b = [capped_b4[c // 4][:, c % 4, :] for c in range(TILES)]
-        size = {}
-        z_rows = [held("z_rows_%d" % b, [P, 4, BANK], BF16) for b in range(2)]
+        z_rows = [held("z_rows_%d" % b, [P, 4, 2, P, 2], BF16) for b in range(2)]
         z_q = {}
 
-        def pick_b(c, b_t, j0, j1):
-            nc.vector.tensor_copy(capped_b[c][:, j0:j1], b_t[:].indirect(pos2_t[:, j0 // 16 : j1 // 16]))
+        def cap(c, size, j0, j1):
+            nc.scalar.activation(size, picked_a[c][:, j0:j1], ACT.Abs)
+            for term in (capped_d[c][:, j0:j1], capped_b[c][:, j0:j1]):
+                nc.vector.tensor_tensor(term, term, size, ALU.min)
 
-        def cap_d(c):
-            size[c] = size4[c // 4][:, c % 4, :]
-            nc.scalar.activation(size[c][:], picked_a[c][:], ACT.Abs)
-            nc.vector.tensor_tensor(capped_d[c][:], capped_d[c][:], size[c][:], ALU.min)
-
-        def cap_b(c, j0, j1):
-            nc.vector.tensor_tensor(capped_b[c][:, j0:j1], capped_b[c][:, j0:j1], size[c][:, j0:j1], ALU.min)
-
-        def join(c, j0, j1, turn):
+        def join(c, j0, j1):
             width = j1 - j0
             capped = capped_b[c][:, j0:j1]
-            if c < 6:
-                bank = psum.tile([P, 4, P], F32, name="z_sum", tag="product", bufs=6)
-            else:
-                bank = psum.tile([P, 4, P], F32, name="z_sum", tag="turn_%d" % turn)
+            bank = psum.tile([P, 4, P], F32, name="z_sum", tag="product", bufs=6)
             for i in range(width // P):
                 for first, term in (
                     (True, capped[:, P * i : P * (i + 1)]),
@@ -238,7 +225,8 @@ def tile_list_ballast_treatment_join_kernel(
         def z_out(c, bank, j0, j1):
             blocks = (j1 - j0) // P
             nc.scalar.copy(
-                z_rows[c // 4][:, j0 // P : j1 // P, P * (c % 4) : P * (c % 4 + 1)], bank[:, 0:blocks, :]
+                z_rows[c // 4][:, j0 // P : j1 // P, :, 32 * (c % 4) : 32 * (c % 4 + 1), :],
+                bank[:, 0:blocks, :].rearrange("p i (q u e) -> p i u q e", u=2, e=2),
             )
 
         def z_turn(b, h):
@@ -246,64 +234,65 @@ def tile_list_ballast_treatment_join_kernel(
             i0 = 2 * h
             bank = psum.tile([P, 2, 2, P], F32, name="z_words", tag="turn_%d" % ((b + h) % 2))
             for i in range(2):
-                words = rows[:, i0 + i, :].bitcast(F32)
                 for u in range(2):
-                    nc.tensor.transpose(bank[:, i, u, :], words[:, u : 2 * P : 2], identity[:])
+                    words = rows[:, i0 + i, u, :, :].rearrange("p q e -> p (q e)").bitcast(F32)
+                    nc.tensor.transpose(bank[:, i, u, :], words, identity[:])
             grouped = held("z_grouped_%d_%d" % (b, h), [P, HALF, 4], BF16)
             nc.scalar.copy(
                 grouped[:].bitcast(F32).rearrange("p (i j) u -> p i j u", i=2),
                 bank[:].rearrange("p i u j -> p i j u"),
             )
-            z_q[b, h] = quantise("z_%d_%d" % (b, h), grouped)
+            z_q[b, h] = (held("z_codes_%d_%d" % (b, h), [P, HALF], U32), held("z_scales_%d_%d" % (b, h), [P, HALF], U8))
+            quantise(z_q[b, h][0][:], z_q[b, h][1][:], grouped[:])
 
         def finish(h, w4_q):
             j_cols = slice(HALF * h, HALF * (h + 1))
-            staged4 = ring.tile([P, 4, 2, HALF], F32, name="staged", tag="slot_%d" % (3 * h), align_bytes=64)
-            for c0 in range(0, TILES, 2):
-                bank = psum.tile([P, 2, HALF], F32, name="product", tag="product", bufs=6)
-                staged = staged4[:, c0 // 2, :, :]
-                for i in range(2):
-                    c = c0 + i
-                    cols = slice(P * (c % 4), P * (c % 4 + 1))
-                    for b in (1, 0):
-                        codes, scales = w4_q[2 * (c // 4) + b]
-                        nc.tensor.matmul_mx(
-                            out=bank[:, i, :], lhsT=codes[:, cols].bitcast(FP8X4), lhsT_scale=scales[:, cols],
-                            rhs=z_q[b, h][0][:].bitcast(FP8X4), rhs_scale=z_q[b, h][1][:],
-                            start=(b == 1), stop=(b == 0),
-                        )
-                for i in range(2):
-                    c = c0 + i
-                    nc.vector.scalar_tensor_tensor(
-                        staged[:, i, :], picked_a[c][:, j_cols], minus_ga[:, c : c + 1], bank[:, i, :],
-                        ALU.mult, ALU.add,
+            staged = ring.tile([P, TILES, HALF], F32, name="staged", tag="slot_%d" % (3 * h), align_bytes=64)
+            for c in range(TILES):
+                bank = psum.tile([P, HALF], F32, name="product", tag="product", bufs=6)
+                cols = slice(P * (c % 4), P * (c % 4 + 1))
+                for b in (1, 0):
+                    codes, scales = w4_q[2 * (c // 4) + b]
+                    nc.tensor.matmul_mx(
+                        out=bank[:], lhsT=codes[:, cols].bitcast(FP8X4), lhsT_scale=scales[:, cols],
+                        rhs=z_q[b, h][0][:].bitcast(FP8X4), rhs_scale=z_q[b, h][1][:],
+                        start=(b == 1), stop=(b == 0),
                     )
-                nc.sync.dma_start(out.rearrange("(c p) j -> p c j", p=P)[:, c0 : c0 + 2, j_cols], staged)
+                nc.vector.scalar_tensor_tensor(
+                    staged[:, c, :], picked_a[c][:, j_cols], minus_ga[:, c : c + 1], bank[:], ALU.mult, ALU.add
+                )
+                if c % 2 == 1:
+                    nc.sync.dma_start(
+                        out.rearrange("(c p) j -> p c j", p=P)[:, c - 1 : c + 1, j_cols], staged[:, c - 1 : c + 1, :]
+                    )
 
-        for c in range(TILES + 1):
-            if c < TILES:
-                pick_b(c, b_scores(c), 0, J)
-            if c >= 1:
-                cap_d(c - 1)
-                cap_b(c - 1, 0, J)
         for c in range(TILES - 1):
-            z_out(c, join(c, 0, J, c % 2), 0, J)
-            if c == 3:
-                for h in range(2):
-                    z_turn(0, h)
+            nc.vector.tensor_copy(capped_b[c], b_scores(c)[:].indirect(pos2_t[:]))
+            if c >= 1:
+                cap(c - 1, size4[(c - 1) // 4][:, (c - 1) % 4, :], 0, J)
+        cap(TILES - 2, size4[1][:, 2, :], 0, J)
+        nc.vector.tensor_copy(capped_b[TILES - 1], b_scores(TILES - 1)[:].indirect(pos2_t[:]))
         for h in range(2):
-            z_out(TILES - 1, join(TILES - 1, HALF * h, HALF * (h + 1), 1 - h), HALF * h, HALF * (h + 1))
+            cap(TILES - 1, last_size[h][:], HALF * h, HALF * (h + 1))
+        for c in range(TILES - 1):
+            z_out(c, join(c, 0, J), 0, J)
         for h in range(2):
-            z_turn(1, h)
-        w4_planes = ring.tile([P, 2, H], U8, name="w4_planes", tag="slot_%d" % (SZ + 1), align_bytes=64)
-        w4_q = []
-        for g in range(2):
-            codes = held("w4_codes_%d" % g, [P, H], U32)
-            nc.vector.quantize_mx(
-                out=codes[:].bitcast(FP8X4), scales=w4_planes[:, g, :],
-                in_=w4_rounded[g][:].rearrange("p c t -> p (c t)"),
-            )
+            z_out(TILES - 1, join(TILES - 1, HALF * h, HALF * (h + 1)), HALF * h, HALF * (h + 1))
+        for h in range(2):
             for b in range(2):
-                w4_q.append((codes[:, BANK * b : BANK * (b + 1)], w4_planes[:, g, BANK * b : BANK * (b + 1)]))
+                z_turn(b, h)
+        w4_high.append(ring.tile([P, BANK, 4], BF16, name="w4_high_1", tag="last_0", align_bytes=64))
+        round_weight(nc.vector.tensor_copy, w4_high[1][:], w4_raw[3])
+        w4_scales = ring.tile([P, 2, H], U8, name="w4_scales", tag="last_1", align_bytes=64)
+        w4_codes = held("w4_codes", [P, 2, H], U32)
+        quantise(w4_codes[:, 0, :], w4_scales[:, 0, :], w4_low[:])
+        for b in range(2):
+            cols = slice(BANK * b, BANK * (b + 1))
+            quantise(w4_codes[:, 1, cols], w4_scales[:, 1, cols], w4_high[b][:])
+        w4_q = [
+            (w4_codes[:, g, BANK * b : BANK * (b + 1)], w4_scales[:, g, BANK * b : BANK * (b + 1)])
+            for g in range(2)
+            for b in range(2)
+        ]
         finish(0, w4_q)
         finish(1, w4_q)

@@ -19,8 +19,13 @@ ACT = mybir.ActivationFunctionType
 
 P = 128
 BANK = 512
+PASS = 512
 TILES = H // P
+LAST = TILES - 1
 HALF = J // 2
+PER_PASS = PASS // P
+SCORE_TILES = 16
+PRODUCT_BANKS = 6
 
 
 def tile_list_ballast_treatment_join_kernel(
@@ -29,53 +34,51 @@ def tile_list_ballast_treatment_join_kernel(
 ):
     nc = tc.nc
     with ExitStack() as ctx:
-        keep = ctx.enter_context(tc.tile_pool(name="keep", bufs=1))
-        ring = ctx.enter_context(tc.tile_pool(name="ring", bufs=1))
+        sbuf = ctx.enter_context(tc.tile_pool(name="sbuf", bufs=1))
         psum = ctx.enter_context(tc.psum_pool(name="psum", bufs=1))
 
         def held(name, shape, dtype):
-            return keep.tile(shape, dtype, name=name, align_bytes=64)
+            return sbuf.tile(shape, dtype, name=name, align_bytes=64)
+
+        def tenant(room, name, shape, dtype):
+            return sbuf.tile(shape, dtype, name=name, tag=room, align_bytes=64)
+
+        def product_bank(shape):
+            return psum.tile(shape, F32, name="product", tag="product", bufs=PRODUCT_BANKS)
 
         def load_list(name, source):
-            tile = keep.tile([P, source.shape[1]], U16, name=name)
+            tile = sbuf.tile([P, source.shape[1]], U16, name=name)
             nc.sync.dma_start(tile[:], source)
             return tile
 
-        def zeroed(name, shape, tag=None):
-            tile = ring.tile(shape, U8, name=name, tag=tag or name, align_bytes=64)
-            nc.vector.memset(tile[:].bitcast(I32), 0)
-            return tile
-
-        def load_words(words, slot):
-            tile = ring.tile([P, T], I32, name="table", tag="slot_%d" % slot, align_bytes=64)
+        def load_table(room, words):
+            tile = tenant(room, "table", [P, T], I32)
             nc.sync.dma_start(tile[:], words.rearrange("p t i -> p (t i)").bitcast(I32))
             return tile
 
-        def load_scales(tile, scales, rows=range(4)):
-            for r in rows:
+        def load_planes(planes, scales):
+            for r in range(4):
                 nc.sync.dma_start(
-                    tile[r:P:32].bitcast(I32), scales[:, r:16:4, :].rearrange("a q c -> q a c").bitcast(I32)
+                    planes[r:P:32].bitcast(I32), scales[:, r:16:4, :].rearrange("n q c -> q n c").bitcast(I32)
                 )
 
-        def load_stacked_scales(tile, scales):
-            for q in range(4):
-                nc.sync.dma_start(
-                    tile[32 * q : 32 * q + 8, :].bitcast(I32), scales[:, 4 * q : 4 * q + 4, :].bitcast(I32)
-                )
+        def load_weight(room, rows):
+            tile = tenant(room, "weight", [P, 4, BANK], F32)
+            nc.sync.dma_start(tile[:], rows.rearrange("(p t) c -> p t c", t=4))
+            return tile
+
+        def load_w4(room, quarter):
+            g, n = divmod(quarter, 2)
+            return load_weight(room, w4[PASS * n : PASS * (n + 1), BANK * g : BANK * (g + 1)])
 
         def gather_words(name, table, offsets):
             tile = held(name, [P, S], U32)
             nc.vector.tensor_copy(tile[:], table[:].bitcast(U32).indirect(offsets[:]))
             return tile
 
-        def gather_scales(name, table, offsets):
+        def gather_scales(name, plane, offsets):
             tile = held(name, [P, S], U8)
-            nc.vector.tensor_copy(tile[:], table.indirect(offsets[:]))
-            return tile
-
-        def load_weight(rows, slot):
-            tile = ring.tile([P, 4, BANK], F32, name="weight", tag="slot_%d" % slot, align_bytes=64)
-            nc.sync.dma_start(tile[:], rows.rearrange("(p t) c -> p t c", t=4))
+            nc.vector.tensor_copy(tile[:], plane.indirect(offsets[:]))
             return tile
 
         def round_weight(copy, rounded, raw):
@@ -84,215 +87,217 @@ def tile_list_ballast_treatment_join_kernel(
         def quantise(codes, scales, rounded):
             nc.vector.quantize_mx(out=codes.bitcast(FP8X4), scales=scales, in_=rounded.rearrange("p c t -> p (c t)"))
 
-        def scores(passes):
-            tile = ring.tile([P, S], F32, name="scores", tag="scores", bufs=16, align_bytes=64)
+        def scores(tile, passes):
             for m0 in range(0, S, BANK):
-                cols = slice(m0, m0 + BANK)
-                bank = psum.tile([P, BANK], F32, name="product", tag="product", bufs=6)
-                for a, (w_codes, w_scales, v_codes, v_scales) in enumerate(passes):
+                entries = slice(m0, m0 + BANK)
+                bank = product_bank([P, BANK])
+                for n, (weight_codes, weight_scales, entry_codes, entry_scales) in enumerate(passes):
                     nc.tensor.matmul_mx(
-                        out=bank[:], lhsT=w_codes, lhsT_scale=w_scales,
-                        rhs=v_codes[:, cols].bitcast(FP8X4), rhs_scale=v_scales[:, cols],
-                        start=(a == 0), stop=(a == len(passes) - 1),
+                        out=bank[:], lhsT=weight_codes, lhsT_scale=weight_scales,
+                        rhs=entry_codes[:, entries].bitcast(FP8X4), rhs_scale=entry_scales[:, entries],
+                        start=(n == 0), stop=(n == len(passes) - 1),
                     )
-                nc.scalar.copy(tile[:, cols], bank[:])
+                nc.scalar.copy(tile[:, entries], bank[:])
             return tile
 
-        tab3_plane = zeroed("tab3_plane", [P, 1, T])
-        tab_plane = zeroed("tab_plane", [P, 1, T])
-        tab2_plane = zeroed("tab2_plane", [P, T])
-        w3_plane = zeroed("w3_plane", [P, 1, H])
-        w2_plane = zeroed("w2_plane", [P, 2, H], "last_1")
-        v2_scales_1 = zeroed("v2_scales_1", [P, S])
-        identity = held("identity", [P, P], F32)
+        def score_tile():
+            return sbuf.tile([P, S], F32, name="scores", tag="scores", bufs=SCORE_TILES, align_bytes=64)[:]
+
+        tab3_plane = held("tab3_plane", [P, 1, T], U8)
+        w3_plane = held("w3_plane", [P, 1, H], U8)
+        tab_plane = held("tab_plane", [P, 1, T], U8)
+        for plane in (tab3_plane, w3_plane, tab_plane):
+            nc.vector.memset(plane[:].bitcast(I32), 0)
         ga_rows = held("ga_rows", [P, P], F32)
         nc.gpsimd.memset(ga_rows[:], 0.0)
+        identity = held("identity", [P, P], F32)
         make_identity(nc, identity[:])
+        tab2_planes = held("tab2_planes", [P, T], U8)
+        w2_planes = tenant("late_1", "w2_planes", [P, 2, H], U8)
+        v2_plane_1 = held("v2_plane_1", [P, S], U8)
+        for plane in (tab2_planes, w2_planes, v2_plane_1):
+            nc.gpsimd.memset(plane[:].bitcast(I32), 0)
 
-        def load_w4(i):
-            g, b = divmod(i, 2)
-            return load_weight(w4[b * BANK : (b + 1) * BANK, g * BANK : (g + 1) * BANK], i)
-
-        offs_t = load_list("offs", offs)
-        offs3_t = load_list("offs3", offs3)
-        tab_t = load_words(tab_words[0], 0)
-        offs2_t = load_list("offs2", offs2)
+        offs3_tile = load_list("offs3", offs3)
+        offs_tile = load_list("offs", offs)
+        offs2_tile = load_list("offs2", offs2)
+        load_planes(tab3_plane, tab3_scales)
+        tab3_tile = load_table("big_0", tab3_words[0])
         nc.sync.dma_start(ga_rows[0:TILES, :], ga.rearrange("(c p) -> c p", p=P))
-        load_scales(tab3_plane, tab3_scales)
-        w1_raw = [load_weight(w1[:, 0:BANK], 1)]
-        load_scales(tab_plane, tab_scales, range(3))
-        w1_raw.append(load_weight(w1[:, BANK:H], 2))
-        load_scales(tab_plane, tab_scales, range(3, 4))
-        tab3_t = load_words(tab3_words[0], 3)
-        load_stacked_scales(tab2_plane, tab2_scales)
-        tab2_t = [load_words(tab2_words[a], 4 + a) for a in range(2)]
-        pos1_t = load_list("pos1", pos1)
-        w3_t = held("w3", [P, H], I32)
-        nc.sync.dma_start(w3_t[:], w3_words[0].rearrange("p c i -> p (c i)").bitcast(I32))
-        load_scales(w3_plane, w3_scales)
-        pos3_t = load_list("pos3", pos3)
-        pos2_t = load_list("pos2", pos2)
+        load_planes(w3_plane, w3_scales)
+        w3_codes = held("w3_codes", [P, H], I32)
+        nc.sync.dma_start(w3_codes[:], w3_words[0].rearrange("p c i -> p (c i)").bitcast(I32))
+        load_planes(tab_plane, tab_scales)
+        tab_tile = load_table("big_3", tab_words[0])
+        pos3_tile = load_list("pos3", pos3)
+        w1_raw = [load_weight("big_%d" % (1 + g), w1[:, BANK * g : BANK * (g + 1)]) for g in range(2)]
 
-        v_codes = gather_words("v_codes", tab_t, offs_t)
-        v3_scales = gather_scales("v3_scales", tab3_plane[:, 0, :], offs3_t)
-        minus_ga = held("minus_ga", [P, TILES], F32)
-        ga_bank = psum.tile([P, P], F32, name="ga_bank", tag="turn_0")
+        v3_scales = gather_scales("v3_scales", tab3_plane[:, 0, :], offs3_tile)
+        v3_codes = gather_words("v3_codes", tab3_tile, offs3_tile)
+        v_scales = gather_scales("v_scales", tab_plane[:, 0, :], offs_tile)
+        v_codes = gather_words("v_codes", tab_tile, offs_tile)
+
+        for quadrant in range(4):
+            nc.sync.dma_start(
+                tab2_planes[32 * quadrant : 32 * quadrant + 8, :].bitcast(I32),
+                tab2_scales[:, 4 * quadrant : 4 * quadrant + 4, :].bitcast(I32),
+            )
+        tab2_tiles = [load_table(room, tab2_words[n]) for n, room in enumerate(("big_0", "big_3"))]
+        w2_codes = tenant("late_0", "w2_codes", [P, 2, 2 * H], U8)
+        nc.sync.dma_start(w2_codes[:].bitcast(I32), w2_words.rearrange("n p c -> p n c").bitcast(I32))
+        pos1_tile = load_list("pos1", pos1)
+        pos2_tile = load_list("pos2", pos2)
+        load_planes(w2_planes, w2_scales)
+
+        ga_bank = psum.tile([P, P], F32, name="ga_bank", tag="words_0")
         nc.tensor.transpose(ga_bank[:], ga_rows[:], identity[:])
+        minus_ga = held("minus_ga", [P, TILES], F32)
         nc.scalar.mul(minus_ga[:], ga_bank[:, 0:TILES], -1.0)
-        w1_rounded = ring.tile([P, H, 4], BF16, name="w1_rounded", tag="rounded", align_bytes=64)
-        w1_codes = held("w1_codes", [P, H], U32)
-        w1_scales = held("w1_scales", [P, H], U8)
+
+        terms = [held("terms_%d" % c, [P, 2, J], F32) for c in range(TILES)]
+
+        def pick_d(c, tile):
+            rows = slice(P * c, P * (c + 1))
+            scores(tile, [(w3_codes[:, rows].bitcast(FP8X4), w3_plane[:, 0, rows], v3_codes, v3_scales)])
+            nc.vector.tensor_copy(terms[c][:, 0, :], tile.indirect(pos3_tile[:]))
+
+        for c in range(TILES - 2):
+            pick_d(c, score_tile())
+
+        w1_rounded = tenant("rounded", "w1_rounded", [P, H, 4], BF16)
         for g in range(2):
-            cols = slice(BANK * g, BANK * (g + 1))
-            round_weight(nc.scalar.copy, w1_rounded[:, cols, :], w1_raw[g])
-            quantise(w1_codes[:, cols], w1_scales[:, cols], w1_rounded[:, cols, :])
-        v_scales = gather_scales("v_scales", tab_plane[:, 0, :], offs_t)
-        v3_codes = gather_words("v3_codes", tab3_t, offs3_t)
-        v2_scales = gather_scales("v2_scales", tab2_plane[:], offs2_t)
-        w4_raw = [load_w4(0)]
-        w2_t = ring.tile([P, 2, 2 * H], U8, name="w2", tag="last_0", align_bytes=64)
-        nc.sync.dma_start(w2_t[:].bitcast(I32), w2_words.rearrange("a p c -> p a c").bitcast(I32))
-        load_scales(w2_plane, w2_scales)
+            round_weight(nc.scalar.copy, w1_rounded[:, BANK * g : BANK * (g + 1), :], w1_raw[g])
+        w1_codes = held("w1_codes", [P, H], U32)
+        w1_plane = held("w1_plane", [P, H], U8)
+        quantise(w1_codes[:], w1_plane[:], w1_rounded[:])
+        d_pair = tenant("big_2", "d_pair", [P, 2, S], F32)
+        for i in range(2):
+            pick_d(TILES - 2 + i, d_pair[:, i, :])
+
+        v2_planes = gather_scales("v2_planes", tab2_planes[:], offs2_tile)
+        w4_raw = [load_w4("big_1", 0)]
         for r in range(4):
-            nc.sync.dma_start(v2_scales_1[r:P:32, :].bitcast(I32), v2_scales[4 + r : P : 32, :].bitcast(I32))
-        w4_raw.extend(load_w4(i) for i in range(1, 4))
-        v2_codes = [gather_words("v2_codes_%d" % a, tab2_t[a], offs2_t) for a in range(2)]
+            nc.sync.dma_start(v2_plane_1[r:P:32, :].bitcast(I32), v2_planes[4 + r : P : 32, :].bitcast(I32))
+        w4_raw.append(load_w4("big_2", 1))
+        v2_codes = [gather_words("v2_codes_%d" % n, tab2_tiles[n], offs2_tile) for n in range(2)]
+        w4_raw.extend([load_w4("big_0", 2), load_w4("big_3", 3)])
 
-        picked_a = []
+        a1 = [held("a1_%d" % c, [P, J], F32) for c in range(TILES)]
         for c in range(TILES):
-            cols = slice(P * c, P * (c + 1))
-            a_t = scores([(w1_codes[:, cols].bitcast(FP8X4), w1_scales[:, cols], v_codes, v_scales)])
-            picked = held("picked_a_%d" % c, [P, J], F32)
-            nc.vector.tensor_copy(picked[:], a_t[:].indirect(pos1_t[:]))
-            picked_a.append(picked)
+            rows = slice(P * c, P * (c + 1))
+            tile = scores(score_tile(), [(w1_codes[:, rows].bitcast(FP8X4), w1_plane[:, rows], v_codes, v_scales)])
+            nc.vector.tensor_copy(a1[c][:], tile.indirect(pos1_tile[:]))
 
-        capped_d = []
-        for c in range(TILES):
-            cols = slice(P * c, P * (c + 1))
-            d_t = scores([(w3_t[:, cols].bitcast(FP8X4), w3_plane[:, 0, cols], v3_codes, v3_scales)])
-            capped = held("capped_d_%d" % c, [P, J], F32)
-            nc.vector.tensor_copy(capped[:], d_t[:].indirect(pos3_t[:]))
-            capped_d.append(capped)
-        w4_low = ring.tile([P, H, 4], BF16, name="w4_low", tag="rounded", align_bytes=64)
-        w4_high = [held("w4_high_0", [P, BANK, 4], BF16)]
-        round_weight(nc.scalar.copy, w4_low[:, 0:BANK, :], w4_raw[0])
-        round_weight(nc.scalar.copy, w4_low[:, BANK:H, :], w4_raw[1])
-        round_weight(nc.scalar.copy, w4_high[0][:], w4_raw[2])
+        w4_rounded_01 = tenant("rounded", "w4_rounded_01", [P, 2 * BANK, 4], BF16)
+        for n in range(2):
+            round_weight(nc.scalar.copy, w4_rounded_01[:, BANK * n : BANK * (n + 1), :], w4_raw[n])
 
         def b_scores(c):
             return scores(
+                score_tile(),
                 [
                     (
-                        w2_t[:, a, 2 * P * c : 2 * P * (c + 1)].bitcast(FP4X4),
-                        w2_plane[:, a, P * c : P * (c + 1)],
-                        v2_codes[a],
-                        (v2_scales, v2_scales_1)[a],
+                        w2_codes[:, n, 2 * P * c : 2 * P * (c + 1)].bitcast(FP4X4),
+                        w2_planes[:, n, P * c : P * (c + 1)],
+                        v2_codes[n],
+                        (v2_planes, v2_plane_1)[n],
                     )
-                    for a in range(2)
-                ]
+                    for n in range(2)
+                ],
             )
 
-        capped_b4 = [
-            ring.tile([P, 4, J], F32, name="capped_b", tag="slot_%d" % (4 + i), align_bytes=64) for i in range(2)
-        ]
-        size4 = [ring.tile([P, 4, J], F32, name="size", tag="slot_%d" % (1 + i), align_bytes=64) for i in range(2)]
-        last_size = [
-            ring.tile([P, HALF], F32, name="last_size", tag="last_%d" % h, align_bytes=64) for h in range(2)
-        ]
-        capped_b = [capped_b4[c // 4][:, c % 4, :] for c in range(TILES)]
-        z_rows = [held("z_rows_%d" % b, [P, 4, 2, P, 2], BF16) for b in range(2)]
-        z_q = {}
+        def pick_b(c, tile, j0, j1):
+            nc.vector.tensor_copy(terms[c][:, 1, j0:j1], tile.indirect(pos2_tile[:, j0 // 16 : j1 // 16]))
 
         def cap(c, size, j0, j1):
-            nc.scalar.activation(size, picked_a[c][:, j0:j1], ACT.Abs)
-            for term in (capped_d[c][:, j0:j1], capped_b[c][:, j0:j1]):
-                nc.vector.tensor_tensor(term, term, size, ALU.min)
+            nc.scalar.activation(size, a1[c][:, j0:j1], ACT.Abs)
+            both = terms[c][:, :, j0:j1]
+            nc.vector.tensor_tensor(both, both, size.unsqueeze(1).to_broadcast([P, 2, j1 - j0]), ALU.min)
 
-        def join(c, j0, j1):
-            width = j1 - j0
-            capped = capped_b[c][:, j0:j1]
-            bank = psum.tile([P, 4, P], F32, name="z_sum", tag="product", bufs=6)
-            for i in range(width // P):
-                for first, term in (
-                    (True, capped[:, P * i : P * (i + 1)]),
-                    (False, capped_d[c][:, j0 + P * i : j0 + P * (i + 1)]),
-                ):
-                    nc.tensor.matmul(
-                        bank[:, i, :], lhsT=term, rhs=identity[:], is_transpose=True, start=first, stop=not first
-                    )
-            return bank
+        sizes_low = tenant("big_2", "sizes_low", [P, PER_PASS, J], F32)
+        pick_b(0, b_scores(0), 0, J)
+        for c in range(2):
+            pick_b(c + 1, b_scores(c + 1), 0, J)
+            cap(c, sizes_low[:, c, :], 0, J)
+        w4_rounded_2 = held("w4_rounded_2", [P, BANK, 4], BF16)
+        round_weight(nc.scalar.copy, w4_rounded_2[:], w4_raw[2])
+        sizes_high = tenant("big_0", "sizes_high", [P, PER_PASS, J], F32)
+        for c in range(2, LAST - 1):
+            pick_b(c + 1, b_scores(c + 1), 0, J)
+            cap(c, (sizes_low, sizes_high)[c // PER_PASS][:, c % PER_PASS, :], 0, J)
+        cap(LAST - 1, sizes_high[:, (LAST - 1) % PER_PASS, :], 0, J)
+        last_b = b_scores(LAST)
+        for half in range(2):
+            pick_b(LAST, last_b, HALF * half, HALF * (half + 1))
+        for half in range(2):
+            last_size = tenant("late_%d" % half, "last_size", [P, HALF], F32)
+            cap(LAST, last_size[:], HALF * half, HALF * (half + 1))
 
-        def z_out(c, bank, j0, j1):
+        z_pairs = [held("z_pairs_%d" % n, [P, J // P, 2, P, 2], BF16) for n in range(2)]
+
+        def add_terms(c, j0, j1):
             blocks = (j1 - j0) // P
+            bank = product_bank([P, J // P, P])
+            for block in range(blocks):
+                for term in (1, 0):
+                    nc.tensor.matmul(
+                        bank[:, block, :], lhsT=terms[c][:, term, j0 + P * block : j0 + P * (block + 1)],
+                        rhs=identity[:], is_transpose=True, start=(term == 1), stop=(term == 0),
+                    )
+            first = 32 * (c % PER_PASS)
             nc.scalar.copy(
-                z_rows[c // 4][:, j0 // P : j1 // P, :, 32 * (c % 4) : 32 * (c % 4 + 1), :],
-                bank[:, 0:blocks, :].rearrange("p i (q u e) -> p i u q e", u=2, e=2),
+                z_pairs[c // PER_PASS][:, j0 // P : j1 // P, :, first : first + 32, :],
+                bank[:, 0:blocks, :].rearrange("j block (q u e) -> j block u q e", u=2, e=2),
             )
 
-        def z_turn(b, h):
-            rows = z_rows[b]
-            i0 = 2 * h
-            bank = psum.tile([P, 2, 2, P], F32, name="z_words", tag="turn_%d" % ((b + h) % 2))
-            for i in range(2):
+        def quantise_z(n, half):
+            bank = psum.tile([P, 2, 2, P], F32, name="z_words", tag="words_%d" % ((n + half) % 2))
+            for block in range(2):
                 for u in range(2):
-                    words = rows[:, i0 + i, u, :, :].rearrange("p q e -> p (q e)").bitcast(F32)
-                    nc.tensor.transpose(bank[:, i, u, :], words, identity[:])
-            grouped = held("z_grouped_%d_%d" % (b, h), [P, HALF, 4], BF16)
+                    words = z_pairs[n][:, 2 * half + block, u, :, :].rearrange("j p e -> j (p e)").bitcast(F32)
+                    nc.tensor.transpose(bank[:, block, u, :], words, identity[:])
+            rounded = held("z_rounded_%d_%d" % (n, half), [P, HALF, 4], BF16)
             nc.scalar.copy(
-                grouped[:].bitcast(F32).rearrange("p (i j) u -> p i j u", i=2),
-                bank[:].rearrange("p i u j -> p i j u"),
+                rounded[:].bitcast(F32).rearrange("p (block j) u -> p block j u", block=2),
+                bank[:].rearrange("p block u j -> p block j u"),
             )
-            z_q[b, h] = (held("z_codes_%d_%d" % (b, h), [P, HALF], U32), held("z_scales_%d_%d" % (b, h), [P, HALF], U8))
-            quantise(z_q[b, h][0][:], z_q[b, h][1][:], grouped[:])
+            codes = held("z_codes_%d_%d" % (n, half), [P, HALF], U32)
+            plane = held("z_plane_%d_%d" % (n, half), [P, HALF], U8)
+            quantise(codes[:], plane[:], rounded[:])
+            return codes, plane
 
-        def finish(h, w4_q):
-            j_cols = slice(HALF * h, HALF * (h + 1))
-            staged = ring.tile([P, TILES, HALF], F32, name="staged", tag="slot_%d" % (3 * h), align_bytes=64)
+        for c in range(LAST):
+            add_terms(c, 0, J)
+        for half in range(2):
+            add_terms(LAST, HALF * half, HALF * (half + 1))
+        z_operands = [[quantise_z(n, half) for n in range(2)] for half in range(2)]
+
+        w4_rounded_3 = tenant("late_0", "w4_rounded_3", [P, BANK, 4], BF16)
+        round_weight(nc.vector.tensor_copy, w4_rounded_3[:], w4_raw[3])
+        w4_planes = tenant("late_1", "w4_planes", [P, 4 * BANK], U8)
+        w4_codes = held("w4_codes", [P, 4 * BANK], U32)
+        quantise(w4_codes[:, 0 : 2 * BANK], w4_planes[:, 0 : 2 * BANK], w4_rounded_01[:])
+        for quarter, rounded in ((2, w4_rounded_2), (3, w4_rounded_3)):
+            columns = slice(BANK * quarter, BANK * (quarter + 1))
+            quantise(w4_codes[:, columns], w4_planes[:, columns], rounded[:])
+
+        out_tiles = out.rearrange("(c p) j -> p c j", p=P)
+        for half, room in enumerate(("big_1", "big_3")):
+            joined = slice(HALF * half, HALF * (half + 1))
+            result = tenant(room, "result", [P, TILES, HALF], F32)
             for c in range(TILES):
-                bank = psum.tile([P, HALF], F32, name="product", tag="product", bufs=6)
-                cols = slice(P * (c % 4), P * (c % 4 + 1))
-                for b in (1, 0):
-                    codes, scales = w4_q[2 * (c // 4) + b]
+                bank = product_bank([P, HALF])
+                for n in (1, 0):
+                    first = BANK * (2 * (c // PER_PASS) + n) + P * (c % PER_PASS)
+                    z_codes, z_plane = z_operands[half][n]
                     nc.tensor.matmul_mx(
-                        out=bank[:], lhsT=codes[:, cols].bitcast(FP8X4), lhsT_scale=scales[:, cols],
-                        rhs=z_q[b, h][0][:].bitcast(FP8X4), rhs_scale=z_q[b, h][1][:],
-                        start=(b == 1), stop=(b == 0),
+                        out=bank[:], lhsT=w4_codes[:, first : first + P].bitcast(FP8X4),
+                        lhsT_scale=w4_planes[:, first : first + P],
+                        rhs=z_codes[:].bitcast(FP8X4), rhs_scale=z_plane[:],
+                        start=(n == 1), stop=(n == 0),
                     )
                 nc.vector.scalar_tensor_tensor(
-                    staged[:, c, :], picked_a[c][:, j_cols], minus_ga[:, c : c + 1], bank[:], ALU.mult, ALU.add
+                    result[:, c, :], a1[c][:, joined], minus_ga[:, c : c + 1], bank[:], ALU.mult, ALU.add
                 )
                 if c % 2 == 1:
-                    nc.sync.dma_start(
-                        out.rearrange("(c p) j -> p c j", p=P)[:, c - 1 : c + 1, j_cols], staged[:, c - 1 : c + 1, :]
-                    )
-
-        for c in range(TILES - 1):
-            nc.vector.tensor_copy(capped_b[c], b_scores(c)[:].indirect(pos2_t[:]))
-            if c >= 1:
-                cap(c - 1, size4[(c - 1) // 4][:, (c - 1) % 4, :], 0, J)
-        cap(TILES - 2, size4[1][:, 2, :], 0, J)
-        nc.vector.tensor_copy(capped_b[TILES - 1], b_scores(TILES - 1)[:].indirect(pos2_t[:]))
-        for h in range(2):
-            cap(TILES - 1, last_size[h][:], HALF * h, HALF * (h + 1))
-        for c in range(TILES - 1):
-            z_out(c, join(c, 0, J), 0, J)
-        for h in range(2):
-            z_out(TILES - 1, join(TILES - 1, HALF * h, HALF * (h + 1)), HALF * h, HALF * (h + 1))
-        for h in range(2):
-            for b in range(2):
-                z_turn(b, h)
-        w4_high.append(ring.tile([P, BANK, 4], BF16, name="w4_high_1", tag="last_0", align_bytes=64))
-        round_weight(nc.vector.tensor_copy, w4_high[1][:], w4_raw[3])
-        w4_scales = ring.tile([P, 2, H], U8, name="w4_scales", tag="last_1", align_bytes=64)
-        w4_codes = held("w4_codes", [P, 2, H], U32)
-        quantise(w4_codes[:, 0, :], w4_scales[:, 0, :], w4_low[:])
-        for b in range(2):
-            cols = slice(BANK * b, BANK * (b + 1))
-            quantise(w4_codes[:, 1, cols], w4_scales[:, 1, cols], w4_high[b][:])
-        w4_q = [
-            (w4_codes[:, g, BANK * b : BANK * (b + 1)], w4_scales[:, g, BANK * b : BANK * (b + 1)])
-            for g in range(2)
-            for b in range(2)
-        ]
-        finish(0, w4_q)
-        finish(1, w4_q)
+                    nc.sync.dma_start(out_tiles[:, c - 1 : c + 1, joined], result[:, c - 1 : c + 1, :])

from contextlib import ExitStack

import concourse.mybir as mybir
from concourse.masks import make_identity

K, K2, K3, H, T, S, J = 512, 1024, 512, 1024, 2048, 1024, 512
FLOPS = 2 * (K + K2 + K3) * H * S + 2 * H * H * J

F32 = mybir.dt.float32
BF16 = mybir.dt.bfloat16
I32 = mybir.dt.int32
U32 = mybir.dt.uint32
U16 = mybir.dt.uint16
U8 = mybir.dt.uint8
FP8X4 = mybir.dt.float8_e4m3fn_x4
FP4X4 = mybir.dt.float4_e2m1fn_x4
ALU = mybir.AluOpType
ACT = mybir.ActivationFunctionType

P = 128
BANK = 512
PASS = 512
TILES = H // P
LAST = TILES - 1
HALF = J // 2
PER_PASS = PASS // P
SCORE_TILES = 16
PRODUCT_BANKS = 6


def tile_list_ballast_treatment_join_kernel(
    tc, tab_words, tab_scales, tab2_words, tab2_scales, tab3_words, tab3_scales, offs, offs2, offs3,
    pos1, pos2, pos3, w1, w2_words, w2_scales, w3_words, w3_scales, w4, ga, out,
):
    nc = tc.nc
    with ExitStack() as ctx:
        sbuf = ctx.enter_context(tc.tile_pool(name="sbuf", bufs=1))
        psum = ctx.enter_context(tc.psum_pool(name="psum", bufs=1))

        def held(name, shape, dtype):
            return sbuf.tile(shape, dtype, name=name, align_bytes=64)

        def tenant(room, name, shape, dtype):
            return sbuf.tile(shape, dtype, name=name, tag=room, align_bytes=64)

        def product_bank(shape):
            return psum.tile(shape, F32, name="product", tag="product", bufs=PRODUCT_BANKS)

        def load_list(name, source):
            tile = sbuf.tile([P, source.shape[1]], U16, name=name)
            nc.sync.dma_start(tile[:], source)
            return tile

        def load_table(room, words):
            tile = tenant(room, "table", [P, T], I32)
            nc.sync.dma_start(tile[:], words.rearrange("p t i -> p (t i)").bitcast(I32))
            return tile

        def load_planes(planes, scales):
            for r in range(4):
                nc.sync.dma_start(
                    planes[r:P:32].bitcast(I32), scales[:, r:16:4, :].rearrange("n q c -> q n c").bitcast(I32)
                )

        def load_weight(room, rows):
            tile = tenant(room, "weight", [P, 4, BANK], F32)
            nc.sync.dma_start(tile[:], rows.rearrange("(p t) c -> p t c", t=4))
            return tile

        def load_w4(room, quarter):
            g, n = divmod(quarter, 2)
            return load_weight(room, w4[PASS * n : PASS * (n + 1), BANK * g : BANK * (g + 1)])

        def gather_words(name, table, offsets):
            tile = held(name, [P, S], U32)
            nc.vector.tensor_copy(tile[:], table[:].bitcast(U32).indirect(offsets[:]))
            return tile

        def gather_scales(name, plane, offsets):
            tile = held(name, [P, S], U8)
            nc.vector.tensor_copy(tile[:], plane.indirect(offsets[:]))
            return tile

        def round_weight(copy, rounded, raw):
            copy(rounded.rearrange("p (c i) t -> p c t i", i=4), raw[:].rearrange("p t (c i) -> p c t i", i=4))

        def quantise(codes, scales, rounded):
            nc.vector.quantize_mx(out=codes.bitcast(FP8X4), scales=scales, in_=rounded.rearrange("p c t -> p (c t)"))

        def scores(tile, passes):
            for m0 in range(0, S, BANK):
                entries = slice(m0, m0 + BANK)
                bank = product_bank([P, BANK])
                for n, (weight_codes, weight_scales, entry_codes, entry_scales) in enumerate(passes):
                    nc.tensor.matmul_mx(
                        out=bank[:], lhsT=weight_codes, lhsT_scale=weight_scales,
                        rhs=entry_codes[:, entries].bitcast(FP8X4), rhs_scale=entry_scales[:, entries],
                        start=(n == 0), stop=(n == len(passes) - 1),
                    )
                nc.scalar.copy(tile[:, entries], bank[:])
            return tile

        def score_tile():
            return sbuf.tile([P, S], F32, name="scores", tag="scores", bufs=SCORE_TILES, align_bytes=64)[:]

        tab3_plane = held("tab3_plane", [P, 1, T], U8)
        w3_plane = held("w3_plane", [P, 1, H], U8)
        tab_plane = held("tab_plane", [P, 1, T], U8)
        for plane in (tab3_plane, w3_plane, tab_plane):
            nc.vector.memset(plane[:].bitcast(I32), 0)
        ga_rows = held("ga_rows", [P, P], F32)
        nc.gpsimd.memset(ga_rows[:], 0.0)
        identity = held("identity", [P, P], F32)
        make_identity(nc, identity[:])
        tab2_planes = held("tab2_planes", [P, T], U8)
        w2_planes = tenant("late_1", "w2_planes", [P, 2, H], U8)
        v2_plane_1 = held("v2_plane_1", [P, S], U8)
        for plane in (tab2_planes, w2_planes, v2_plane_1):
            nc.gpsimd.memset(plane[:].bitcast(I32), 0)

        offs3_tile = load_list("offs3", offs3)
        offs_tile = load_list("offs", offs)
        offs2_tile = load_list("offs2", offs2)
        load_planes(tab3_plane, tab3_scales)
        tab3_tile = load_table("big_0", tab3_words[0])
        nc.sync.dma_start(ga_rows[0:TILES, :], ga.rearrange("(c p) -> c p", p=P))
        load_planes(w3_plane, w3_scales)
        w3_codes = held("w3_codes", [P, H], I32)
        nc.sync.dma_start(w3_codes[:], w3_words[0].rearrange("p c i -> p (c i)").bitcast(I32))
        load_planes(tab_plane, tab_scales)
        tab_tile = load_table("big_3", tab_words[0])
        pos3_tile = load_list("pos3", pos3)
        w1_raw = [load_weight("big_%d" % (1 + g), w1[:, BANK * g : BANK * (g + 1)]) for g in range(2)]

        v3_scales = gather_scales("v3_scales", tab3_plane[:, 0, :], offs3_tile)
        v3_codes = gather_words("v3_codes", tab3_tile, offs3_tile)
        v_scales = gather_scales("v_scales", tab_plane[:, 0, :], offs_tile)
        v_codes = gather_words("v_codes", tab_tile, offs_tile)

        for quadrant in range(4):
            nc.sync.dma_start(
                tab2_planes[32 * quadrant : 32 * quadrant + 8, :].bitcast(I32),
                tab2_scales[:, 4 * quadrant : 4 * quadrant + 4, :].bitcast(I32),
            )
        tab2_tiles = [load_table(room, tab2_words[n]) for n, room in enumerate(("big_0", "big_3"))]
        w2_codes = tenant("late_0", "w2_codes", [P, 2, 2 * H], U8)
        nc.sync.dma_start(w2_codes[:].bitcast(I32), w2_words.rearrange("n p c -> p n c").bitcast(I32))
        pos1_tile = load_list("pos1", pos1)
        pos2_tile = load_list("pos2", pos2)
        load_planes(w2_planes, w2_scales)

        ga_bank = psum.tile([P, P], F32, name="ga_bank", tag="words_0")
        nc.tensor.transpose(ga_bank[:], ga_rows[:], identity[:])
        minus_ga = held("minus_ga", [P, TILES], F32)
        nc.scalar.mul(minus_ga[:], ga_bank[:, 0:TILES], -1.0)

        terms = [held("terms_%d" % c, [P, 2, J], F32) for c in range(TILES)]

        def pick_d(c, tile):
            rows = slice(P * c, P * (c + 1))
            scores(tile, [(w3_codes[:, rows].bitcast(FP8X4), w3_plane[:, 0, rows], v3_codes, v3_scales)])
            nc.vector.tensor_copy(terms[c][:, 0, :], tile.indirect(pos3_tile[:]))

        for c in range(TILES - 2):
            pick_d(c, score_tile())

        w1_rounded = tenant("rounded", "w1_rounded", [P, H, 4], BF16)
        for g in range(2):
            round_weight(nc.scalar.copy, w1_rounded[:, BANK * g : BANK * (g + 1), :], w1_raw[g])
        w1_codes = held("w1_codes", [P, H], U32)
        w1_plane = held("w1_plane", [P, H], U8)
        quantise(w1_codes[:], w1_plane[:], w1_rounded[:])
        d_pair = tenant("big_2", "d_pair", [P, 2, S], F32)
        for i in range(2):
            pick_d(TILES - 2 + i, d_pair[:, i, :])

        v2_planes = gather_scales("v2_planes", tab2_planes[:], offs2_tile)
        w4_raw = [load_w4("big_1", 0)]
        for r in range(4):
            nc.sync.dma_start(v2_plane_1[r:P:32, :].bitcast(I32), v2_planes[4 + r : P : 32, :].bitcast(I32))
        w4_raw.append(load_w4("big_2", 1))
        v2_codes = [gather_words("v2_codes_%d" % n, tab2_tiles[n], offs2_tile) for n in range(2)]
        w4_raw.extend([load_w4("big_0", 2), load_w4("big_3", 3)])

        a1 = [held("a1_%d" % c, [P, J], F32) for c in range(TILES)]
        for c in range(TILES):
            rows = slice(P * c, P * (c + 1))
            tile = scores(score_tile(), [(w1_codes[:, rows].bitcast(FP8X4), w1_plane[:, rows], v_codes, v_scales)])
            nc.vector.tensor_copy(a1[c][:], tile.indirect(pos1_tile[:]))

        w4_rounded_01 = tenant("rounded", "w4_rounded_01", [P, 2 * BANK, 4], BF16)
        for n in range(2):
            round_weight(nc.scalar.copy, w4_rounded_01[:, BANK * n : BANK * (n + 1), :], w4_raw[n])

        def b_scores(c):
            return scores(
                score_tile(),
                [
                    (
                        w2_codes[:, n, 2 * P * c : 2 * P * (c + 1)].bitcast(FP4X4),
                        w2_planes[:, n, P * c : P * (c + 1)],
                        v2_codes[n],
                        (v2_planes, v2_plane_1)[n],
                    )
                    for n in range(2)
                ],
            )

        def pick_b(c, tile, j0, j1):
            nc.vector.tensor_copy(terms[c][:, 1, j0:j1], tile.indirect(pos2_tile[:, j0 // 16 : j1 // 16]))

        def cap(c, size, j0, j1):
            nc.scalar.activation(size, a1[c][:, j0:j1], ACT.Abs)
            both = terms[c][:, :, j0:j1]
            nc.vector.tensor_tensor(both, both, size.unsqueeze(1).to_broadcast([P, 2, j1 - j0]), ALU.min)

        sizes_low = tenant("big_2", "sizes_low", [P, PER_PASS, J], F32)
        pick_b(0, b_scores(0), 0, J)
        for c in range(2):
            pick_b(c + 1, b_scores(c + 1), 0, J)
            cap(c, sizes_low[:, c, :], 0, J)
        w4_rounded_2 = held("w4_rounded_2", [P, BANK, 4], BF16)
        round_weight(nc.scalar.copy, w4_rounded_2[:], w4_raw[2])
        sizes_high = tenant("big_0", "sizes_high", [P, PER_PASS, J], F32)
        for c in range(2, LAST - 1):
            pick_b(c + 1, b_scores(c + 1), 0, J)
            cap(c, (sizes_low, sizes_high)[c // PER_PASS][:, c % PER_PASS, :], 0, J)
        cap(LAST - 1, sizes_high[:, (LAST - 1) % PER_PASS, :], 0, J)
        last_b = b_scores(LAST)
        for half in range(2):
            pick_b(LAST, last_b, HALF * half, HALF * (half + 1))
        for half in range(2):
            last_size = tenant("late_%d" % half, "last_size", [P, HALF], F32)
            cap(LAST, last_size[:], HALF * half, HALF * (half + 1))

        z_pairs = [held("z_pairs_%d" % n, [P, J // P, 2, P, 2], BF16) for n in range(2)]

        def add_terms(c, j0, j1):
            blocks = (j1 - j0) // P
            bank = product_bank([P, J // P, P])
            for block in range(blocks):
                for term in (1, 0):
                    nc.tensor.matmul(
                        bank[:, block, :], lhsT=terms[c][:, term, j0 + P * block : j0 + P * (block + 1)],
                        rhs=identity[:], is_transpose=True, start=(term == 1), stop=(term == 0),
                    )
            first = 32 * (c % PER_PASS)
            nc.scalar.copy(
                z_pairs[c // PER_PASS][:, j0 // P : j1 // P, :, first : first + 32, :],
                bank[:, 0:blocks, :].rearrange("j block (q u e) -> j block u q e", u=2, e=2),
            )

        def quantise_z(n, half):
            bank = psum.tile([P, 2, 2, P], F32, name="z_words", tag="words_%d" % ((n + half) % 2))
            for block in range(2):
                for u in range(2):
                    words = z_pairs[n][:, 2 * half + block, u, :, :].rearrange("j p e -> j (p e)").bitcast(F32)
                    nc.tensor.transpose(bank[:, block, u, :], words, identity[:])
            rounded = held("z_rounded_%d_%d" % (n, half), [P, HALF, 4], BF16)
            nc.scalar.copy(
                rounded[:].bitcast(F32).rearrange("p (block j) u -> p block j u", block=2),
                bank[:].rearrange("p block u j -> p block j u"),
            )
            codes = held("z_codes_%d_%d" % (n, half), [P, HALF], U32)
            plane = held("z_plane_%d_%d" % (n, half), [P, HALF], U8)
            quantise(codes[:], plane[:], rounded[:])
            return codes, plane

        for c in range(LAST):
            add_terms(c, 0, J)
        for half in range(2):
            add_terms(LAST, HALF * half, HALF * (half + 1))
        z_operands = [[quantise_z(n, half) for n in range(2)] for half in range(2)]

        w4_rounded_3 = tenant("late_0", "w4_rounded_3", [P, BANK, 4], BF16)
        round_weight(nc.vector.tensor_copy, w4_rounded_3[:], w4_raw[3])
        w4_planes = tenant("late_1", "w4_planes", [P, 4 * BANK], U8)
        w4_codes = held("w4_codes", [P, 4 * BANK], U32)
        quantise(w4_codes[:, 0 : 2 * BANK], w4_planes[:, 0 : 2 * BANK], w4_rounded_01[:])
        for quarter, rounded in ((2, w4_rounded_2), (3, w4_rounded_3)):
            columns = slice(BANK * quarter, BANK * (quarter + 1))
            quantise(w4_codes[:, columns], w4_planes[:, columns], rounded[:])

        out_tiles = out.rearrange("(c p) j -> p c j", p=P)
        for half, room in enumerate(("big_1", "big_3")):
            joined = slice(HALF * half, HALF * (half + 1))
            result = tenant(room, "result", [P, TILES, HALF], F32)
            for c in range(TILES):
                bank = product_bank([P, HALF])
                for n in (1, 0):
                    first = BANK * (2 * (c // PER_PASS) + n) + P * (c % PER_PASS)
                    z_codes, z_plane = z_operands[half][n]
                    nc.tensor.matmul_mx(
                        out=bank[:], lhsT=w4_codes[:, first : first + P].bitcast(FP8X4),
                        lhsT_scale=w4_planes[:, first : first + P],
                        rhs=z_codes[:].bitcast(FP8X4), rhs_scale=z_plane[:],
                        start=(n == 1), stop=(n == 0),
                    )
                nc.vector.scalar_tensor_tensor(
                    result[:, c, :], a1[c][:, joined], minus_ga[:, c : c + 1], bank[:], ALU.mult, ALU.add
                )
                if c % 2 == 1:
                    nc.sync.dma_start(out_tiles[:, c - 1 : c + 1, joined], result[:, c - 1 : c + 1, :])
